import numpy as np, ml_dtypes
CORES = [9,25,41,57]
N = 4
BF = ml_dtypes.bfloat16
def gentries(a):
    return np.ascontiguousarray(a.reshape(8, 16, -1).transpose(0, 2, 1)).reshape(8, -1)
def gtable(e):
    e = np.asarray(e); return np.ascontiguousarray(e.reshape(8, -1, 16).transpose(0, 2, 1)).reshape(128, -1).astype(np.int32)
V, E, RO, TH = 4096, 512, 4, 8
S, M, F = 16 * N, RO * E, RO * E // N
U = np.arange(V)
ROOM = min(V // 2 - E, V // 20)
def graph(rng, full=()):
    A = np.full((8, 16, V), V, np.int64); place = np.argsort(rng.random((8, V)), axis=1)
    near = rng.random((8, 16)) < 0.7; near[np.arange(RO), np.arange(RO)] = True
    for g in full: near[g] = True
    for g in range(8):
        mk = np.argsort(rng.random((V // 32, 31)), axis=1)[:, :16] + 1
        for i in range(16):
            if near[g, i]:
                A[g, i, place[g]] = place[g][U ^ mk[U // 32, i]]
            else:
                o = rng.permutation(V); A[g, i, o[0::2]] = o[1::2]; A[g, i, o[1::2]] = o[0::2]
    return A, place
def thin(rng, A, most):
    for g in range(8):
        for i in range(16):
            p = A[g, i]; lo = np.nonzero((p < V) & (U < p) & (U > 0) & (p != V - 1))[0]
            d = rng.permutation(lo)[:int(rng.integers(0, most[i] + 1))]; e = p[d]
            A[g, i, d] = V; A[g, i, e] = V
    return A
def tests(rng, A, first, again):
    tv = np.zeros((8, RO, E), np.int64)
    for g in range(8):
        seen = np.zeros(V)
        for t in range(RO):
            p = A[g, t]; lo = np.nonzero((p < V) & (U < p))[0]
            key = rng.random(len(lo)) - first[g, lo] - first[g, p[lo]] - again * (seen[lo] + seen[p[lo]])
            lo = rng.permutation(lo[np.argsort(key)[:E]])
            tv[g, t] = np.where(rng.random(E) < 0.5, p[lo], lo)
            seen = np.zeros(V); seen[lo] = 1; seen[p[lo]] = 1
    return tv
def cloud(rng, place, lams):
    c = V // 32; n = lambda *s: rng.standard_normal(s, dtype=np.float32)
    lam = rng.choice(np.array(lams, np.float32), (8, 1, c, 1)); ld = (rng.random((8, 1, c, 32)) * 2 - 1).astype(np.float32)
    w = 128 + 25 * n(8, S, c, 1) + 60 * lam * ld * n(8, S, c, 1) + 20 * n(8, S, c, 32)
    w = np.clip(np.rint(w), 0, 255).astype(np.int64).reshape(8, S, V)
    step = rng.choice(np.array([1, 1, 1, 16, 64]), (8, 1, V)); w = w // step * step
    return np.take_along_axis(w, np.argsort(place, axis=1)[:, None, :], 2)
def pack(s, A, tv):
    return {"x": np.ascontiguousarray(s.reshape(8, N, 16, V).transpose(1, 0, 2, 3)).reshape(N, 128, V).astype(np.float32).astype(BF),
            "adj": np.stack([A.reshape(128, V).astype(np.int32)] * N), "tv": np.stack([gtable(tv.reshape(8, M))] * N)}
def setup_inputs(rng):
    A, place = graph(rng); A = thin(rng, A, [ROOM] * 16)
    return pack(cloud(rng, place, [0, 0, 0.3, 1]), A, tests(rng, A, np.zeros((8, V)), 0))
def setup_inputs_edge(rng):
    A, place = graph(rng); A = thin(rng, A, [ROOM] * 16)
    ty = rng.random((8, 1, V)); low = ty < 0.2; high = (ty >= 0.2) & (ty < 0.4)
    lv = np.where(low, rng.integers(40, 110, (8, 1, V)), rng.integers(190, 240, (8, 1, V)))
    goal = rng.choice(np.array([TH, TH - 1, -TH, 1 - TH] + [TH + 1] * 8 + [-TH - 1] * 8 + [TH + 2] * 4 + [-TH - 2] * 4 + [S - 2] * 2), (8, 1, V))
    tie = (S - goal) % 2; nb = (S - tie - goal) // 2
    o = np.argsort(np.argsort(rng.random((8, S - 1, V), dtype=np.float32), axis=1), axis=1)
    run = rng.random((8, 1, V)); k = np.arange(S - 1)[None, :, None]
    o = np.where(run < 0.35, S - 2 - k, np.where(run < 0.6, k, o))
    out = np.where(rng.random((8, S - 1, V), dtype=np.float32) < 0.5, 10, 250)
    rest = np.where(low | high, lv, np.where(o < nb, 150, out))
    head = np.where(low, 100, np.where(high, lv, np.where(tie == 1, 100, 250)))
    s = np.concatenate([head, rest], axis=1)
    return pack(s, A, tests(rng, A, (low | high)[:, 0].astype(np.float64), 0))
def setup_inputs_alike(rng):
    A, place = graph(rng, (0, 6, 7)); o = place[7, :32 * (V // 128)]; A[7][:, o] = A[7, 0, o]
    A = thin(rng, A, [ROOM] * 16); A[1::2, 8:] = A[1::2, :8]
    A[::6, 1] = A[::6, 0]; A[6, 9:] = A[6, 8]
    s = cloud(rng, place, [0, 0.3, 1]); s[2:6] = 255 * (rng.random((4, S, V)) < 0.5)
    for g in (0, 7):
        p = A[g, 15]; lo = np.nonzero((p < V) & (U < p))[0]; lo = rng.permutation(lo)[:V // 20]; s[g][:, p[lo]] = s[g][:, lo]
    return pack(s, A, tests(rng, A, np.zeros((8, V)), 0))
def setup_inputs_bare(rng):
    A, place = graph(rng); A = thin(rng, A, [ROOM] * RO + [V // 2] * (16 - RO))
    A[1, RO:15] = V; A[2, RO:] = V; A[6, RO + 1:] = V
    s = cloud(rng, place, [0, 0, 0.3, 1]); first = np.zeros((8, V)); first[:, 0] = 1; first[:, V - 1] = 1
    for g in range(8):
        for c in (0, V - 1):
            y = int(A[g, RO, c])
            if y < V:
                s[g][:, c] = s[g][:, y]; first[g, y] = 1
    return pack(s, A, tests(rng, A, first, 0))
def setup_inputs_chain(rng):
    A, place = graph(rng, (5, 6)); A = thin(rng, A, [ROOM] * 16)
    s = cloud(rng, place, [0.3, 0.6, 1])
    s[5] = rng.integers(0, 256, (S, 1))
    s[6] = rng.integers(0, 256, (S, V)); p = A[6, 1]; lo = np.nonzero((p < V) & (U < p))[0]; s[6][:, p[lo]] = s[6][:, lo]
    return pack(s, A, tests(rng, A, np.zeros((8, V)), 1))
def setup_inputs_spread(rng):
    A, place = graph(rng); A = thin(rng, A, [ROOM] * 16)
    s = np.floor(np.exp2(8 * rng.random((8, 1, V))) * rng.random((8, S, V))) * (rng.random((8, 1, V)) > 0.0625)
    return pack(s.astype(np.int64), A, tests(rng, A, np.zeros((8, V)), 0))
def check_inputs(d):
    bad = []; xf = d["x"].astype(np.float32)
    if not np.all((xf >= 0) & (xf <= 255) & (np.floor(xf) == xf)): bad.append("range of x")
    for k, hi in (("adj", V), ("tv", V - 1)):
        if np.min(d[k]) < 0 or np.max(d[k]) > hi: bad.append("range of " + k)
        if np.any(d[k] != d[k][:1]): bad.append(k + " alike on all ranks")
    if "range of adj" in bad or "range of tv" in bad: return bad
    A = d["adj"][0].astype(np.int64).reshape(8, 16, V); B = np.concatenate([A, np.full((8, 16, 1), V, np.int64)], axis=2)
    if not np.all((A == V) | ((np.take_along_axis(B, A, 2) == U) & (A != U))): bad.append("partners are mutual")
    vs = gentries(d["tv"][0]).astype(np.int64).reshape(8, RO, E); g8 = np.arange(8)[:, None]
    for t in range(RO):
        v = vs[:, t]; y = A[g8, t, v]; both = np.sort(np.concatenate([v, y], axis=1), axis=1)
        if np.any(y >= V) or np.any(both[:, 1:] == both[:, :-1]): bad.append("ends of round " + str(t))
    return bad
def reference(x, adj, tv):
    A = adj[0].astype(np.int64).reshape(8, 16, V)
    s = np.ascontiguousarray(x.astype(np.float32).astype(np.int32).reshape(N, 8, 16, V).transpose(1, 0, 2, 3)).reshape(8, S, V)
    vs = gentries(tv[0]).astype(np.int64).reshape(8, RO, E); ys = np.zeros((8, RO, E), np.int64); sp = np.full((8, RO, E), V, np.int64)
    g8 = np.arange(8)[:, None]; g3 = np.arange(8)[:, None, None]; i3 = np.arange(16)[None, :, None]
    for t in range(RO):
        v = vs[:, t]; y = A[g8, t, v]; ys[:, t] = y
        z = A[g3, i3, y[:, None, :]]
        zz = np.where(z < V, z, 0); a = np.zeros((8, 16, E), np.int64)
        xv = np.take_along_axis(s, v[:, None, :], 2); xy = np.take_along_axis(s, y[:, None, :], 2)
        for i in range(16):
            xz = np.take_along_axis(s, zz[:, i][:, None, :], 2)
            a[:, i] = np.sum(np.sign((xv - xz) * (xy - xz)), axis=1)
        ok = (z < V) & (z != v[:, None, :]) & (np.abs(a) <= TH)
        hit = np.any(ok, axis=1); i1 = np.argmax(ok, axis=1)
        sp[:, t] = np.where(hit, np.take_along_axis(z, i1[:, None, :], 1)[:, 0], V)
        A[g8, t, v] = np.where(hit, V, y); A[g8, t, y] = np.where(hit, V, v)
    v = vs.reshape(8, 1, M); y = ys.reshape(8, 1, M); se = sp.reshape(8, 1, M)
    w = A[g3, i3, y]; ww = np.where(w < V, w, 0); inside = np.zeros((8, 16, M), bool)
    for i in range(16): inside = inside | (A[g3, i, ww] == v)
    fl = (se < V) & (w < V) & inside & (w != se)
    return {"ysep": np.stack([sp.reshape(8, M)] * N).astype(np.float32),
            "yflag": np.stack([fl[:, :, r * F:(r + 1) * F].reshape(128, F) for r in range(N)]).astype(np.float32).astype(BF)}

@@ -1,0 +1,688 @@
+from concourse.bass import DstId, RemoteDMATransfer
+from concourse.mybir import AluOpType as OP, ActivationFunctionType as AF
+
+NR, E = 4, 512
+ND = 4
+BF, U2, F4, F2, I4 = "bfloat16", "uint16", "float32", "float16", "int32"
+SCRATCH = {}
+for _n, _w, _d in (
+        ("adjs", 4096, I4), ("xs", 4112, BF), ("tvs", 128, I4), ("tvu", 128, U2), ("ones", 128, BF),
+        ("c1", 8, BF), ("c2", 8, BF), ("b1", 128, BF), ("bm", 128, BF), ("im", 128, BF), ("lt", 128, BF),
+        ("ev", 128, BF), ("od", 128, BF), ("dp", 128, BF), ("dm", 128, BF), ("de", 128, BF), ("do", 128, BF),
+        ("s00", 128, F2), ("s01", 128, F2), ("s10", 128, F2), ("s11", 128, F2), ("ut", 512, F2), ("cjf", 512, F2),
+        ("q16", 128, BF), ("qm", 128, BF), ("hi", 128, BF), ("nhi", 128, BF), ("ni", 128, BF), ("pi", 128, BF), ("pn", 128, BF),
+        ("imf", 128, F2), ("nif", 128, F2), ("nbm", 128, F2), ("b2k", 128, F2), ("bcb", 2048, BF), ("bch", 2048, F2),
+        ("gall", 2048, BF), ("gp", 512, BF), ("gn", 512, BF), ("zj", 128, F2), ("zz", 128, F2), ("tlf", 128, F2),
+        ("zv", 32, F2), ("vj", 32, U2), ("cvj", 512, U2), ("lv", 128, U2), ("lvi", 128, I4), ("mvi", 128, I4), ("mv", 128, U2),
+        ("sf", 512, F2), ("mt_", 8192, BF), ("eqs", 512, BF), ("nh", 512, BF), ("fl", 512, BF), ("wsum", 256, BF),
+        ("ok", 256, BF), ("first", 256, F2), ("fz", 256, F2), ("tj", 128, U2), ("tl", 128, U2), ("mint", 512, U2),
+        ("eq", 2048, BF), ("inv", 2048, BF), ("lki", 512, I4), ("yli", 128, I4), ("mini", 512, I4), ("ce", 2048, F2),
+        ("cj", 2048, U2), ("li", 2048, U2), ("zc", 2048, F2), ("h", 16384, BF), ("part", 2048, BF), ("pin", 3584, BF),
+        ("sepin", 2048, U2), ("sepf", 2048, F4), ("rv", 2048, BF), ("mg", 2048, BF), ("rk", 8192, BF), ("xv", 1024, BF),
+        ("xy", 1024, BF), ("m", 2048, F4), ("hh", 1024, BF), ("d", 1024 * ND, BF), ("w", 3072, BF), ("s", 3072, BF)):
+    SCRATCH[_n] = ("sbuf", [128, _w], _d)
+for _n, _w in (("psT", 2048), ("psA", 512), ("psX", 512), ("psW", 1024)):
+    SCRATCH[_n] = ("psum", [128, _w], F4)
+
+SEMAPHORES = ["cv", "ca", "cp", "cg", "ltv", "ladj", "lx", "loc", "svj", "slv", "oflag", "brr3"]
+for _t in range(NR):
+    SEMAPHORES += ["%s%d" % (_k, _t) for _k in ("arr", "sar", "stj", "stl", "mdp", "osep")]
+    SEMAPHORES += ["sli%d_%d" % (_t, _k) for _k in range(8)]
+
+CY, GA, SC, PE = 0.9e-3, 1.5, 2.8, 0.43e-3
+WAKE, LAT = 0.05, 2.2
+LATE = 20.0
+LAND = {"arr": 3.0, "sar": 4.0, "brr": 4.0}
+
+
+def rank_program(g, core, T, topo):
+    r = T.rank_of(core)
+    if r is None:
+        return
+    eng = {"v": g.vector, "a": g.scalar, "p": g.tensor, "g": g, "s": g.sync}
+    tasks = []
+    bonus, lift = {}, [0.0]
+
+    def op(e, fn, reads, writes, cost):
+        bonus[len(tasks)] = lift[0]
+        tasks.append((e, "op", fn, "c" + e, 1, reads, writes, cost, cost))
+
+    def dma(e, sem, out, in_, reads, writes, lat=LAT, first=0.0):
+        bonus[len(tasks)] = first
+        tasks.append((e, "dma", lambda q: q.dma_start(out, in_), sem, 16, reads, writes, 0.1, lat))
+
+    def ap(rg):
+        return T[rg[0]][:, rg[1]:rg[2]]
+
+    def full(name):
+        return (name, 0, SCRATCH[name][1][1])
+
+    def blk(name, k, w=512):
+        return (name, w * k, w * k + w)
+
+    def part(rg, q, n=4):
+        w = (rg[2] - rg[1]) // n
+        return (rg[0], rg[1] + q * w, rg[1] + q * w + w)
+
+    def small(*rgs):
+        return all(SCRATCH[x[0]][0] == "sbuf" and SCRATCH[x[0]][2] in (BF, U2, F2) for x in rgs)
+
+    def vc(n, f=1.0):
+        return 0.02 + max(64, n * f) * CY
+
+    def copy(e, out, in_):
+        n = in_[2] - in_[1]
+        if e == "v":
+            op("v", lambda q: q.tensor_copy(ap(out), ap(in_)), [in_], [out], vc(n, 0.5 if small(out, in_) else 1))
+        else:
+            op("a", lambda q: q.activation(ap(out), ap(in_), AF.Copy), [in_], [out], 0.05 + n * CY)
+
+    def act(out, in_, func):
+        op("a", lambda q: q.activation(ap(out), ap(in_), func), [in_], [out], 0.05 + (in_[2] - in_[1]) * CY)
+
+    def tt(out, a, b, o):
+        f = 1 if a[0].startswith("ps") or b[0].startswith("ps") else 2
+        op("v", lambda q: q.tensor_tensor(ap(out), ap(a), ap(b), o), [a, b], [out], vc(a[2] - a[1], f))
+
+    def ts(out, a, s1, o1):
+        op("v", lambda q: q.tensor_scalar(ap(out), ap(a), s1, None, o1), [a], [out], vc(a[2] - a[1], 0.5 if small(out, a) else 1))
+
+    def gcost(off):
+        return 0.07 + 16 * (off[2] - off[1]) * GA * CY
+
+    def gather(e, out, win, off):
+        if e == "v":
+            op("v", lambda q: q.tensor_copy(ap(out), ap(win).indirect(ap(off))), [win, off], [out], gcost(off))
+        else:
+            op("a", lambda q: q.activation(ap(out), ap(win).indirect(ap(off)), AF.Copy), [win, off], [out], gcost(off))
+
+    def gather_less(out, win, off):
+        op("v", lambda q: q.tensor_scalar(ap(out), ap(win).indirect(ap(off)), -2048.0, None, OP.add), [win, off], [out], gcost(off))
+
+    def mm(out, lhs, rhs, start, stop, bank=None):
+        op("p", lambda q: q.matmul(ap(out), ap(lhs), ap(rhs), start, stop), [lhs, rhs], [bank or out], 0.03 + (rhs[2] - rhs[1]) * PE)
+
+    def gi(i):
+        return blk("gall", i, 128)
+
+    def tj(t):
+        return blk("tj", t, 32)
+
+    def tl(t):
+        return blk("tl", t, 32)
+
+    def li(t, i, n=1):
+        return ("li", 512 * t + 32 * i, 512 * t + 32 * i + 32 * n)
+
+    def li3(n, i, k=1):
+        return ("li", 1536 + 256 * n + 16 * i, 1536 + 256 * n + 16 * i + 16 * k)
+
+    def hw(t):
+        return blk("h", t, 4096)
+
+    def psz(w=512):
+        return ("psW", 512, 512 + w)
+
+    XW, AW = full("xs"), full("adjs")
+
+    dma("s", "ltv", T.tvs[:, :], T.tv[:, :], [], [full("tvs")], LAT, 1000.0)
+    dma("s", "ladj", T.adjs[:, :], T.adj[:, :], [], [full("adjs")], 7.0, 500.0)
+    dma("s", "lx", T.xs[:, 0:4096], T.x[:, :], [], [("xs", 0, 4096)], 10.0, 400.0)
+
+    def fill(rg, val, cost):
+        op("v", lambda q: q.memset(ap(rg), val), [], [rg], cost)
+
+    lift[0] = 200.0
+    fill(full("ones"), 1.0, 0.1)
+    lift[0] = 0.0
+    fill(full("bcb"), 1.0, 1.0)
+    fill(full("gall"), 0.0, 1.0)
+    fill(("xs", 4096, 4112), 0.0, 0.1)
+
+    def asel(out, in_, pat, cmp, base, cm):
+        op("g", lambda q: q.affine_select(ap(out), ap(in_), pat, cmp, 0.0, base, cm), [in_], [out], 0.2 + 2 * CY * (in_[2] - in_[1]))
+
+    one128 = full("ones")
+    lift[0] = 300.0
+    asel(full("c1"), ("ones", 0, 8), [[-16, 8]], OP.is_ge, 0, 1)
+    asel(full("c2"), full("c1"), [[16, 8]], OP.is_ge, 15, -1)
+    asel(full("im"), one128, [[-1, 128]], OP.is_equal, 0, 1)
+    half = [[0, 4], [-1, 2], [0, 16]]
+    asel(full("ev"), full("im"), half, OP.is_equal, 0, 0)
+    asel(full("od"), full("im"), half, OP.is_equal, 1, 0)
+    asel(full("dp"), one128, [[-1, 128]], OP.is_equal, -16, 1)
+    asel(full("dm"), one128, [[-1, 128]], OP.is_equal, 16, 1)
+    asel(full("de"), full("dp"), half, OP.is_equal, 0, 0)
+    asel(full("do"), full("dm"), half, OP.is_equal, 1, 0)
+    lift[0] = 250.0
+    asel(full("b1"), one128, [[-16, 8], [0, 16]], OP.is_ge, 0, 1)
+    asel(full("bm"), full("b1"), [[16, 8], [0, 16]], OP.is_ge, 15, -1)
+    asel(full("lt"), full("bm"), [[1, 128]], OP.is_gt, 0, -1)
+    lift[0] = 0.0
+    asel(full("bcb"), full("bcb"), [[-1, 16], [-16, 8], [0, 16]], OP.is_equal, 0, 1)
+
+    def zeros(s, *after):
+        op("g", lambda q: q.iota(ap(hw(s)), [[0, 4096]], 0, 0, allow_small_or_imprecise_dtypes=True), list(after), [hw(s)], 7.0)
+
+    for s in range(2):
+        zeros(s, full("lt"))
+
+    def diag(i):
+        op("v", lambda q: q.tensor_copy(T.gall[:, 128 * i + i:128 * i + 128:16], T.c2[:, :]), [full("c2")], [gi(i)], 0.12)
+
+    lift[0] = 200.0
+    copy("v", full("tvu"), full("tvs"))
+    for a, b in (("s00", "ev"), ("s11", "od"), ("s10", "de"), ("s01", "do")):
+        copy("v", full(a), full(b))
+    lift[0] = 0.0
+    for i in range(16):
+        diag(i)
+    for nm, f in (("hi", 0.5), ("nhi", -0.5), ("ni", -1.0), ("pi", 512.0), ("pn", -512.0), ("imf", 1.0), ("nif", -1.0)):
+        ts(full(nm), full("im"), f, OP.mult)
+    ts(full("gp"), ("gall", 0, 512), 64.0, OP.mult)
+    ts(full("gn"), ("gall", 0, 512), -64.0, OP.mult)
+
+    SEL = [["s00", "s01"], ["s10", "s11"]]
+
+    def flip(rows):
+        op("v", lambda q: q.transpose(T.ut[:, :], ap(rows)), [rows], [full("ut")], vc(256))
+
+    def pick(u, h):
+        op("p", lambda q: q.matmul(T.psX[:, 16 * u:16 * u + 16], T[SEL[u][h]][:, :], T.ut[:, 16 * h:512:32], h == 0, h == 1),
+           [full(SEL[u][h]), full("ut")], [("psX", 0, 32)], 0.06)
+
+    def ylist(u):
+        op("v", lambda q: q.tensor_scalar(T.tl[:, u:32:2], T.psX[:, 16 * u:16 * u + 16], 2048.0, None, OP.add),
+           [("psX", 0, 32)], [tl(0)], vc(16))
+
+    def ymix(u):
+        op("v", lambda q: q.tensor_copy(T.tj[:, u:32:2], T.tl[:, 16 * u:16 * u + 16]), [tl(0)], [tj(0)], vc(16))
+
+    def entry(i):
+        op("v", lambda q: q.tensor_scalar(ap(li(0, i)), T.psW[:, i:1024:32], 2048.0, None, OP.add), [full("psW")], [li(0, i)], vc(32))
+
+    def first_lists():
+        gather_less(blk("ce", 0), AW, blk("tvu", 0, 32))
+        flip(blk("ce", 0))
+        for u in range(2):
+            for h in range(2):
+                pick(u, h)
+        for u in range(2):
+            ylist(u)
+        for u in range(2):
+            ymix(u)
+        gather_less(full("cjf"), AW, tj(0))
+        flip(full("cjf"))
+        for u in range(2):
+            for h in range(2):
+                mm(("psW", 512 * u, 512 * u + 496), full(SEL[u][h]), ("ut", 16 * h, 16 * h + 496), h == 0, h == 1)
+        for i in range(1, 16):
+            entry(i)
+
+    def rows_v(t):
+        a, b = 512 * t, 32 * t
+        gather_less(blk("ce", t), AW, blk("tvu", t, 32))
+        for n in range(2):
+            dma("s", "stj%d" % t, T.zj[:, b + 16 * n:b + 16 * n + 16], T.ce[t::16, a + 256 * n:a + 256 * n + 256],
+                [blk("ce", t)], [("zj", b + 16 * n, b + 16 * n + 16)], LAT, 50.0)
+        for n in range(2):
+            dma("s", "stl%d" % t, T.zz[:, b + 16 * n:b + 16 * n + 16], T.ce[t + 16 * n::32, a:a + 512],
+                [blk("ce", t)], [("zz", b + 16 * n, b + 16 * n + 16)], LAT, 40.0)
+
+    def plus(out, a, b, step, src):
+        op("v", lambda q: q.tensor_scalar(T[out][:, a:b:step], ap(src), 2048.0, None, OP.add), [src], [(out, a, b)], vc(16))
+
+    def rows_y(t):
+        b = 32 * t
+        if t == 3:
+            plus("tj", b, b + 32, 1, ("zj", b, b + 32))
+        else:
+            for n in range(2):
+                plus("tj", b + n, b + 32, 2, ("zj", b + 16 * n, b + 16 * n + 16))
+        gather("v", blk("cj", t), AW, tj(t))
+        op("v", lambda q: q.transpose(T.tlf[:, b:b + 32], T.zz[:, b:b + 32]), [("zz", b, b + 32)], [("tlf", b, b + 32)], vc(32))
+        plus("tl", b, b + 32, 1, ("tlf", b, b + 32))
+        rest = [i for i in range(16) if i != t]
+        if t == 3:
+            for n in range(2):
+                for k, i in enumerate(rest):
+                    z = li3(n, i)
+                    dma("s", "sli3_%d" % ((15 * n + k) // 4), ap(z), T.cj[i::16, 1536 + 256 * n:1792 + 256 * n], [blk("cj", t)], [z],
+                        LAT + 0.12 * k)
+            return
+        for n, i in enumerate(rest):
+            dma("s", "sli%d_%d" % (t, n // 4), ap(li(t, i)), T.cj[i::16, 512 * t:512 * t + 512],
+                [blk("cj", t)], [li(t, i)], LAT + 0.12 * n)
+
+    lift[0] = 60.0
+    first_lists()
+    for fn in (rows_v, rows_y):
+        for t in range(1, NR):
+            lift[0] = 60.0 - 5 * t
+            fn(t)
+    lift[0] = 0.0
+
+    def prep(t):
+        b = t % 2
+        xv, xy, hb = blk("xv", b), blk("xy", b), blk("hh", b)
+        gather("a", xv, XW, blk("tvu", t, 32))
+        gather("a", xy, XW, tl(t))
+        mm(full("psX"), full("hi"), xv, True, False)
+        mm(full("psX"), full("hi"), xy, False, True)
+        if t == 3:
+            for n in range(2):
+                m1, m2 = ("m", 1024 + 512 * n, 1280 + 512 * n), ("m", 1280 + 512 * n, 1536 + 512 * n)
+                copy("a", m1, ("psX", 256 * n, 256 * n + 256))
+                dma("s", "mdp3", ap(m2), ap(m1), [m1], [m2], LAT + 0.3)
+        else:
+            m1, m2 = blk("m", 2 * b), blk("m", 2 * b + 1)
+            copy("a", m1, full("psX"))
+            if t:
+                dma("s", "mdp%d" % t, ap(m2), ap(m1), [m1], [m2], LAT + 0.6)
+            else:
+                copy("a", m2, full("psX"))
+        mm(full("psX"), full("hi"), xv, True, False)
+        mm(full("psX"), full("nhi"), xy, False, True)
+        act(hb, full("psX"), AF.Abs)
+
+    def mins(t):
+        n = NR if t == r else t + 1
+        yl = blk("yli", t, 32)
+        copy("v", yl, tl(t))
+        tt(blk("mini", 5 * t, 32), blk("tvs", t, 32), yl, OP.min)
+        if t == 3:
+            for k in range(2):
+                b = 384 + 64 * k
+                copy("v", ("lki", b, b + 48), li3(k, 0, 3))
+                for s in range(3):
+                    tt(part(blk("mini", 12 + s, 32), k, 2), ("lki", b + 16 * s, b + 16 * s + 16), part(yl, k, 2), OP.min)
+        else:
+            for a, b in ((0, t), (t + 1, n)):
+                if a < b:
+                    copy("v", ("lki", 128 * t + 32 * a, 128 * t + 32 * b), li(t, a, b - a))
+                for s in range(a, b):
+                    tt(blk("mini", 4 * t + s, 32), blk("lki", 4 * t + s, 32), yl, OP.min)
+        copy("v", ("mint", 128 * t, 128 * t + 32 * n), ("mini", 128 * t, 128 * t + 32 * n))
+
+    def cols(t):
+        zc, inv, eq, off = blk("zc", t), blk("inv", t), blk("eq", t), tl(t)
+        if t not in (r, 3):
+            zc, inv, off = part(zc, r), part(inv, r), part(off, r)
+        gather_less(zc, AW, off)
+        ts(inv, zc, 2048.0, OP.is_equal)
+        zq = blk("zc", t)
+        if t < 3:
+            zq, eq = part(zq, r), part(eq, r)
+        z = psz(zq[2] - zq[1])
+        mm(z, blk("bch", t, 128), zq, True, True)
+        tt(eq, z, zq, OP.is_equal)
+
+    def bigmats():
+        copy("v", full("bch"), full("bcb"))
+        ts(full("q16"), full("lt"), 16.0, OP.mult)
+        ts(full("nbm"), full("bm"), -1.0, OP.mult)
+        ts(full("b2k"), full("bm"), 2048.0, OP.mult)
+        tt(full("qm"), full("q16"), full("im"), OP.subtract)
+
+    units = []
+    for t in range(NR):
+        ent = [i for i in range(16) if i != t]
+        for c in range(2 if t == 3 else 1):
+            us = []
+            k = 0
+            while k < len(ent):
+                n = 2 if (t or k) and k + 1 < len(ent) and ent[k + 1] == ent[k] + 1 else 1
+                us.append((t, c, ent[k], n))
+                k += n
+            for j, u in enumerate(us):
+                units.append(u + (j == 0, j == len(us) - 1))
+    start = [[n for n, u in enumerate(units) if u[0] == t][0] for t in range(NR)] + [len(units)]
+
+    def unit(n):
+        t, ch, i, k, fst, lst = units[n]
+        wd = 256 if t == 3 else 512
+        c, d0, w0, p0, m0 = wd * k, 1024 * (n % ND), 1024 * (n % 3), 1024 * (n % 2), 1024 * (t % 2) + 512 * ch
+        d, w, s, m, off = ("d", d0, d0 + c), ("w", w0, w0 + c), ("s", w0, w0 + c), ("m", m0, m0 + c), li(t, i, k)
+        hq, acc = blk("hh", t % 2), full("psA")
+        if t == 3:
+            off = li3(ch, i, k)
+            hq = part(hq, ch, 2)
+            acc = ("psX" if ch else "psA", 0, 256)
+        op("v", lambda q: q.tensor_tensor(ap(d), ap(XW).indirect(ap(off)), ap(m), OP.subtract), [XW, off, m], [d], gcost(off))
+        act(w, d, AF.Abs)
+        for j in range(k):
+            o = ("psT", p0 + wd * j, p0 + wd * j + wd)
+            bank = ("psT", p0, p0 + 512) if t == 3 else o
+            mm(o, full("im"), ("w", w0 + wd * j, w0 + wd * j + wd), True, False, bank)
+            mm(o, full("ni"), hq, False, True, bank)
+        act(s, ("psT", p0, p0 + c), AF.Sign)
+        for j in range(k):
+            mm(acc, gi(i + j), ("s", w0 + wd * j, w0 + wd * j + wd), fst and j == 0, lst and j == k - 1)
+
+    others = [q for q in range(NR) if q != r]
+    links = topo.engines(core, T.cores[others[0]])
+
+    def dst(q):
+        a = topo.addr(T.cores[q])
+        return DstId(rid=a[0], pnc=a[1])
+
+    def remote(name, t, transfers, nloc, nrem, src, land):
+        tasks.append(("g", "send", lambda q: q.remote_dma_fused(transfers, local_sem=T.sem.loc), "loc", nloc, [src],
+                      [("token" + name, t, t + 1)], 0.6, 0.6))
+        tasks.append((None, "land", None, name + str(t), 3 * nrem, [("token" + name, t, t + 1)], land, 0.0, LAND[name]))
+
+    def share(t):
+        mine = blk("part", t)
+        copy("a", mine, full("psA"))
+        k = len(links) // 4
+        tr = []
+        for n, q in enumerate(others):
+            mask = sum(1 << e for e in links[n * k:n * k + k])
+            tr.append(RemoteDMATransfer(dst_ids=[dst(q)], dma_engine_mask=mask, remote_sem=T.sem["arr%d" % t],
+                                        srcs=[ap(part(mine, q))], dsts=[ap(part(blk("pin", t), r))]))
+        remote("arr", t, tr, 3 * k, k, mine, [part(blk("pin", t), q) for q in others])
+
+    def pin3(q, a, b):
+        return ("pin", 1536 + 512 * q + a, 1536 + 512 * q + b)
+
+    def share_all(ch):
+        a = 256 * ch
+        mine = ("part", 1536 + a, 1792 + a)
+        copy("a", mine, ("psX" if ch else "psA", 0, 256))
+        name = "brr" if ch else "arr"
+        tr = [RemoteDMATransfer(dst_ids=[dst(q) for q in others], dma_engine_mask=topo.mask(core, T.cores[others[0]]),
+                                remote_sem=T.sem[name + "3"], srcs=[ap(mine)], dsts=[ap(pin3(r, a, a + 256)) for _ in others])]
+        remote(name, 3, tr, len(links), len(links), mine, [pin3(q, a, a + 256) for q in others])
+
+    def rk(t, s):
+        return blk("rk", 4 * t + s)
+
+    def mi(t, s):
+        return blk("mint", 4 * t + s, 32)
+
+    def look(t, s):
+        if t in (r, 3):
+            gather("a", rk(t, s), hw(s), mi(t, s))
+        else:
+            gather("a", part(rk(t, s), r), hw(s), part(mi(t, s), r))
+
+    def decide(t, a, b):
+        def cut(rg):
+            return (rg[0], rg[1] + a, rg[1] + b)
+        w = b - a
+        X, W, K, FI, FZ = [(nm, 0, w) for nm in ("psW", "wsum", "ok", "first", "fz")]
+        mm(X, full("pi"), cut(blk("eq", t)), True, False)
+        mm(X, full("pi"), cut(blk("inv", t)), False, False)
+        for s in range(t):
+            mm(X, blk("gp", s, 128), cut(rk(t, s)), False, False)
+        mm(X, full("im"), cut(blk("part", t)), False, False)
+        for q in others:
+            mm(X, full("im"), pin3(q, a, b) if t == 3 else part(blk("pin", t), q), False, q == others[-1])
+        act(W, X, AF.Abs)
+        ts(K, W, 8.0, OP.is_le)
+        mm(X, full("qm"), K, True, True)
+        ts(FI, X, -1.0, OP.is_equal)
+        tt(FZ, FI, cut(blk("zc", t)), OP.mult)
+        mm(X, full("b2k"), FI, True, False)
+        mm(X, full("nbm"), FZ, False, True)
+        mine = cut(blk("sepin", t))
+        copy("v", mine, X)
+        if t == 3:
+            return
+        tr = [RemoteDMATransfer(dst_ids=[dst(q) for q in others], dma_engine_mask=topo.mask(core, T.cores[others[0]]),
+                                remote_sem=T.sem["sar%d" % t], srcs=[ap(mine)], dsts=[ap(mine) for _ in others])]
+        remote("sar", t, tr, len(links), len(links), mine, [part(blk("sepin", t), q) for q in others])
+
+    def mark(t, a, b):
+        if t == 3 and r == 3:
+            return
+        off, src = ("mint", 160 * t + a // 16, 160 * t + b // 16), ("sepin", 512 * t + a, 512 * t + b)
+        op("v", lambda q: q.tensor_copy(ap(hw(t)).indirect(ap(off)), ap(src)), [off, src], [hw(t)], 0.07 + (b - a) * SC * CY)
+
+    def seps(t, a, b):
+        a, b = 512 * t + a, 512 * t + b
+        out, src = ("sepf", a, b), ("sepin", a, b)
+        op("v", lambda q: q.tensor_scalar(ap(out), ap(src), -1.0, 4096.0, OP.mult, OP.add), [src], [out], vc(b - a))
+        dma("s", "osep%d" % t, T.ysep[:, a:b], T.sepf[0::16, a:b], [out], [])
+
+    def mj(j):
+        return blk("mt_", j)
+
+    def fl_lists():
+        for n in range(2):
+            dma("s", "svj", T.zv[:, 16 * n:16 * n + 16], T.zc[r::16, 512 * r + 256 * n:512 * r + 256 * n + 256],
+                [blk("zc", r)], [("zv", 16 * n, 16 * n + 16)])
+        for n in range(2):
+            plus("vj", n, 32, 2, ("zv", 16 * n, 16 * n + 16))
+        gather("v", full("cvj"), AW, full("vj"))
+        for s in range(NR):
+            dma("s", "slv", ap(blk("lv", s, 32)), T.cvj[s::16, :], [full("cvj")], [blk("lv", s, 32)])
+        copy("v", full("lvi"), full("lv"))
+        for s in range(NR):
+            if s != r:
+                tt(blk("mvi", s, 32), blk("lvi", s, 32), blk("tvs", r, 32), OP.min)
+        for a, b in ((0, r), (r + 1, NR)):
+            if a < b:
+                copy("v", ("mv", 32 * a, 32 * b), ("mvi", 32 * a, 32 * b))
+
+    def match(j):
+        mm(psz(), blk("bch", j, 128), blk("ce", r), True, True)
+        tt(mj(j), psz(), blk("zc", r), OP.is_equal)
+
+    def fl_own(a, b):
+        src, sf, z = ("sepin", 512 * r + a, 512 * r + b), ("sf", a, b), psz(b - a)
+        op("v", lambda q: q.tensor_scalar(ap(sf), ap(src), -1.0, 2048.0, OP.mult, OP.add), [src], [sf], vc((b - a) / 2))
+        mm(z, full("imf"), sf, True, False)
+        mm(z, full("nif"), ("zc", 512 * r + a, 512 * r + b), False, True)
+        ts(("eqs", a, b), z, 0.0, OP.is_equal)
+        ts(("nh", a, b), src, 0.0, OP.is_equal)
+
+    def fl_gather(s):
+        if s != r:
+            gather("v", blk("rv", s), hw(s), blk("mv", s, 32))
+            if s > r:
+                look(r, s)
+
+    def fl_round(s):
+        if s != r:
+            mm(psz(), full("im"), mj(s), True, s == 3)
+            if s == 3:
+                tt(blk("mg", s), psz(), blk("rv", s), OP.is_gt)
+            else:
+                mm(psz(), full("ni"), blk("rv", s), False, True)
+                act(blk("mg", s), psz(), AF.Relu)
+            mm(F, full("im"), blk("mg", s), False, s == 3)
+            if s != 3:
+                mm(F, blk("gn", s, 128), rk(r, s), False, False)
+
+    F = full("psA")
+    mine = (128 * r, 128 * r + 128)
+    for t in range(NR):
+        lift[0] = 20.0 if t else 60.0
+        prep(t)
+        lift[0] = 0.0
+        if t == 0:
+            bigmats()
+            cols(r)
+            for k in range(NR):
+                mins(k)
+                if k != r:
+                    cols(k)
+        for n in range(start[t + 1] - start[t]):
+            unit(start[t] + n)
+            if t and n == 2:
+                for s in range(t - 1):
+                    look(t, s)
+                decide(t - 1, *mine)
+            if t and n == 5:
+                mark(t - 1, 0, 512)
+                look(t, t - 1)
+                seps(t - 1, 0, 512)
+                fl_gather(t - 1)
+            if units[start[t] + n][5] and t == 3:
+                share_all(units[start[t] + n][1])
+        if t == 0:
+            fl_lists()
+            lift[0] = LATE
+            for j in range(16):
+                if j != r:
+                    match(j)
+            lift[0] = 0.0
+        if t < 3:
+            share(t)
+        if t == 0:
+            for s in range(2, NR if r != 3 else 3):
+                zeros(s, ("tokenarr", 0, 1))
+    mm(F, full("pn"), blk("inv", r), True, False)
+    for j in range(4, 16):
+        mm(F, full("im"), mj(j), False, False)
+    for s in range(3):
+        if s != r:
+            fl_round(s)
+    if r != 3:
+        fl_own(0, 512)
+        mm(F, full("pn"), full("eqs"), False, False)
+        mm(F, full("pn"), full("nh"), False, False)
+    for c in range(2):
+        a, b = 256 * c, 256 * c + 256
+        decide(3, a, b)
+        mark(3, a, b)
+        seps(3, a, b)
+        if r == 3:
+            fl_own(a, b)
+    if r != 3:
+        fl_gather(3)
+        mm(F, blk("gn", 3, 128), rk(r, 3), False, False)
+        fl_round(3)
+    else:
+        mm(F, full("pn"), full("nh"), False, False)
+        mm(F, full("pn"), full("eqs"), False, True)
+    ts(full("fl"), F, 0.0, OP.is_gt)
+    dma("s", "oflag", T.yflag[:, :], T.fl[:, :], [full("fl")], [])
+
+    cnt, snap, recs = {}, {}, {}
+    clock = {e: {} for e in eng}
+
+    def wait(e, sem, val, isdma):
+        if isdma:
+            val = cnt[sem]
+        if clock[e].get(sem, 0) >= val:
+            return
+        eng[e].wait_ge(T.sem[sem], val)
+        for k, v in snap.get(sem if isdma else (sem, val), {}).items():
+            if clock[e].get(k, 0) < v:
+                clock[e][k] = v
+        clock[e][sem] = max(clock[e].get(sem, 0), val)
+
+    for x in schedule(tasks, bonus):
+        e, kind, fn, sem, inc, reads, writes, _, _ = tasks[x]
+        reads = [q for q in reads if not q[0].startswith("token")]
+        writes = [q for q in writes if not q[0].startswith("token")]
+        isdma = kind != "op"
+        if kind != "land":
+            best = {}
+            for isw, rgs in ((False, reads), (True, writes)):
+                for buf, a, b in rgs:
+                    for c0, c1, w, e2, s2, v2, d2 in recs.get(buf, []):
+                        if c0 >= b or a >= c1:
+                            continue
+                        if not isw and not w and not (buf.startswith("ps") and e2 != e):
+                            continue
+                        if isw and e2 == e and not d2 and not isdma and (not w or e == "p"):
+                            continue
+                        if s2 not in best or best[s2][0] < v2:
+                            best[s2] = (v2, d2)
+            for s2 in sorted(best, key=lambda z: (best[z][1], z)):
+                wait(e, s2, best[s2][0], best[s2][1])
+        cnt[sem] = cnt.get(sem, 0) + inc
+        if kind == "send":
+            fn(eng[e])
+            continue
+        if kind != "land":
+            fn(eng[e]).then_inc(T.sem[sem], inc)
+            if kind == "op":
+                sn = dict(clock[e])
+                sn[sem] = cnt[sem]
+                snap[(sem, cnt[sem])] = sn
+            else:
+                sn = snap.setdefault(sem, {})
+                for k, v in clock[e].items():
+                    sn[k] = max(sn.get(k, 0), v)
+        for buf, a, b in writes:
+            lst = recs.setdefault(buf, [])
+            lst[:] = [q for q in lst if not (a <= q[0] and q[1] <= b)]
+            lst.append((a, b, True, e, sem, cnt[sem], isdma))
+        for buf, a, b in reads:
+            lst = recs.setdefault(buf, [])
+            lst[:] = [q for q in lst if not (not q[2] and q[4] == sem and a <= q[0] and q[1] <= b)]
+            lst.append((a, b, False, e, sem, cnt[sem], isdma))
+
+    for sem, val in cnt.items():
+        if clock["g"].get(sem, 0) < val:
+            g.wait_ge(T.sem[sem], val)
+            clock["g"][sem] = val
+
+
+def schedule(tasks, bonus):
+    n = len(tasks)
+    deps = [set() for _ in range(n)]
+    recs, group = {}, {}
+    for x in range(n):
+        e, kind, _, sem, _, reads, writes, _, _ = tasks[x]
+        for isw, rgs in ((False, reads), (True, writes)):
+            for buf, a, b in rgs:
+                for c0, c1, w, e2, y in recs.get(buf, []):
+                    if c0 < b and a < c1 and (isw or w or (buf.startswith("ps") and e2 != e)):
+                        deps[x].add(y)
+        for y in list(deps[x]):
+            if tasks[y][1] == "dma":
+                deps[x].update(z for z in group[tasks[y][3]] if z < x)
+        if kind == "dma":
+            group.setdefault(sem, []).append(x)
+        for buf, a, b in writes:
+            lst = recs.setdefault(buf, [])
+            lst[:] = [q for q in lst if not (a <= q[0] and q[1] <= b)]
+            lst.append((a, b, True, e, x))
+        for buf, a, b in reads:
+            recs.setdefault(buf, []).append((a, b, False, e, x))
+        deps[x].discard(x)
+    succ = [[] for _ in range(n)]
+    for x in range(n):
+        for y in deps[x]:
+            succ[y].append(x)
+    prio = [0.0] * n
+    for x in range(n - 1, -1, -1):
+        prio[x] = tasks[x][8] + WAKE + max([prio[y] for y in succ[x]], default=0.0)
+    prio = [prio[x] + bonus.get(x, 0.0) for x in range(n)]
+    left = [len(deps[x]) for x in range(n)]
+    at = [0.0] * n
+    free = {}
+    ready = {}
+    for x in range(n):
+        if not left[x]:
+            ready.setdefault(tasks[x][0], []).append(x)
+    order = []
+    while len(order) < n:
+        pick = None
+        for e in sorted(ready, key=str):
+            lst = ready[e]
+            if not lst:
+                continue
+            f = free.get(e, 0.0)
+            s0 = min(max(f, at[x]) for x in lst)
+            if pick is None or s0 < pick[0]:
+                pick = (s0, e)
+        s0, e = pick
+        x = max((y for y in ready[e] if max(free.get(e, 0.0), at[y]) <= s0 + 0.05), key=lambda y: (prio[y], -y))
+        ready[e].remove(x)
+        st = max(free.get(e, 0.0), at[x])
+        if e is not None:
+            free[e] = st + tasks[x][7]
+        end = st + tasks[x][8] + WAKE
+        order.append(x)
+        for y in succ[x]:
+            at[y] = max(at[y], end)
+            left[y] -= 1
+            if not left[y]:
+                ready.setdefault(tasks[y][0], []).append(y)
+    return order

@@ -1,564 +1,663 @@
 from concourse.bass import DstId, RemoteDMATransfer
 from concourse.mybir import AluOpType as OP, ActivationFunctionType as AF
 
-NR, E = 4, 512
-ND = 4
+NR = 4
+ND = 8
+MATCH = "avavavavavaaaaaa"
+NE = 10
+WAY = "..G.G.G." "G..G..G." "G.G....." "GG.G..:."
+LAG = {".": 0, ":": 0, "g": 4.5, "G": 4.5, "x": 6.5, "X": 6.5}
+LIVE = "aav"
+NEG = "v"
+MK0 = 2
+MK1 = 1
+NW = 7
+PREP = "aaa"
+NF = WAY.count("x") + WAY.count("X")
 BF, U2, F4, F2, I4 = "bfloat16", "uint16", "float32", "float16", "int32"
 SCRATCH = {}
 for _n, _w, _d in (
-        ("adjs", 4096, I4), ("xs", 4112, BF), ("tvs", 128, I4), ("tvu", 128, U2), ("ones", 128, BF),
-        ("c1", 8, BF), ("c2", 8, BF), ("b1", 128, BF), ("bm", 128, BF), ("im", 128, BF), ("lt", 128, BF),
-        ("ev", 128, BF), ("od", 128, BF), ("dp", 128, BF), ("dm", 128, BF), ("de", 128, BF), ("do", 128, BF),
-        ("s00", 128, F2), ("s01", 128, F2), ("s10", 128, F2), ("s11", 128, F2), ("ut", 512, F2), ("cjf", 512, F2),
-        ("q16", 128, BF), ("qm", 128, BF), ("hi", 128, BF), ("nhi", 128, BF), ("ni", 128, BF), ("pi", 128, BF), ("pn", 128, BF),
-        ("imf", 128, F2), ("nif", 128, F2), ("nbm", 128, F2), ("b2k", 128, F2), ("bcb", 2048, BF), ("bch", 2048, F2),
-        ("gall", 2048, BF), ("gp", 512, BF), ("gn", 512, BF), ("zj", 128, F2), ("zz", 128, F2), ("tlf", 128, F2),
-        ("zv", 32, F2), ("vj", 32, U2), ("cvj", 512, U2), ("lv", 128, U2), ("lvi", 128, I4), ("mvi", 128, I4), ("mv", 128, U2),
-        ("sf", 512, F2), ("mt_", 8192, BF), ("eqs", 512, BF), ("nh", 512, BF), ("fl", 512, BF), ("wsum", 256, BF),
-        ("ok", 256, BF), ("first", 256, F2), ("fz", 256, F2), ("tj", 128, U2), ("tl", 128, U2), ("mint", 512, U2),
-        ("eq", 2048, BF), ("inv", 2048, BF), ("lki", 512, I4), ("yli", 128, I4), ("mini", 512, I4), ("ce", 2048, F2),
-        ("cj", 2048, U2), ("li", 2048, U2), ("zc", 2048, F2), ("h", 16384, BF), ("part", 2048, BF), ("pin", 3584, BF),
-        ("sepin", 2048, U2), ("sepf", 2048, F4), ("rv", 2048, BF), ("mg", 2048, BF), ("rk", 8192, BF), ("xv", 1024, BF),
-        ("xy", 1024, BF), ("m", 2048, F4), ("hh", 1024, BF), ("d", 1024 * ND, BF), ("w", 3072, BF), ("s", 3072, BF)):
+        ("xst", 3072, BF), ("xin", 3072, BF), ("xs", 4112, BF), ("tvs", 32, I4), ("tvd", 32, U2),
+        ("adjq", 1024, I4), ("adjh", 1024, F2), ("adjw", 4096, F4), ("ones", 128, BF),
+        ("a0", 128, BF), ("a1", 128, BF), ("pm", 128, BF), ("im", 128, BF), ("b1", 128, BF), ("bm", 128, BF), ("lt", 128, BF),
+        ("k1", 128, BF), ("km", 128, BF), ("z1", 128, BF), ("bz", 192, BF), ("g1", 128, BF), ("gm", 128, BF),
+        ("l1", 128, BF), ("lm", 128, BF), ("r32", 128, BF), ("r16", 16, F4), ("rowm", 8, F4), ("bc", 8, F4),
+        ("gs", 240, BF), ("gs2", 240, BF), ("nbz", 192, BF), ("sel", 2048, BF), ("bch", 2048, BF), ("bs", 384, BF),
+        ("pi", 128, BF), ("hi", 128, BF), ("nhi", 128, BF), ("ni", 128, BF), ("n2", 128, BF),
+        ("q16", 128, BF), ("qm", 128, BF), ("lk", 128, BF), ("pn", 128, BF), ("lpn", 128, BF), ("gp", 128, BF),
+        ("ix", 128, BF), ("ixs", 128, BF), ("v2", 128, BF), ("w1", 8, BF), ("gq", 512, BF), ("sb", 512, BF), ("pn3", 128, BF),
+        ("cv", 512, F2), ("cy", 512, F2), ("ty", 64, F2), ("tz", 512, F2), ("yx", 128, U2), ("yd", 32, U2), ("li", 2048, U2),
+        ("eq", 512, BF), ("inv", 512, BF), ("mt", 8192, BF), ("mk", 4096, BF), ("tb", 4096, BF),
+        ("rk", 512, BF), ("ry", 256, BF), ("rv", 512, BF), ("mg", 2048, BF), ("ok", 128, BF), ("hs", 384, BF),
+        ("tx", 48, F2), ("xl", 48, U2), ("hw", 1040, BF), ("ru", 384, BF),
+        ("fi", 512, F2), ("fz", 512, F2), ("eqs", 512, BF), ("fl", 512, BF), ("flin", 512, BF), ("sepo", 32, F4),
+        ("sepin", 128, F4), ("xv", 1024, BF), ("xy", 1024, BF), ("m", 2048, F4), ("lo", 2048, BF), ("hh", 2048, BF),
+        ("d", 1024 * ND, BF), ("s", 3072, BF), ("w", 1024 * NW, BF), ("nh", 2048, BF), ("rb", 1024 * max(NF, 1), BF)):
     SCRATCH[_n] = ("sbuf", [128, _w], _d)
-for _n, _w in (("psT", 2048), ("psA", 512), ("psX", 512), ("psW", 1024)):
+for _n, _w in (("psT", 2048), ("psA", 1024), ("psF", 512), ("psW", 512)):
     SCRATCH[_n] = ("psum", [128, _w], F4)
 
-SEMAPHORES = ["cv", "ca", "cp", "cg", "ltv", "ladj", "lx", "loc", "svj", "slv", "oflag", "brr3"]
+SEMAPHORES = ["cv", "ca", "cp", "cg", "ltv", "ladj", "lown", "ltb", "loc", "sar", "far", "osep", "oflag"]
 for _t in range(NR):
-    SEMAPHORES += ["%s%d" % (_k, _t) for _k in ("arr", "sar", "stj", "stl", "mdp", "osep")]
-    SEMAPHORES += ["sli%d_%d" % (_t, _k) for _k in range(8)]
+    SEMAPHORES += ["%s%d" % (_k, _t) for _k in ("lx", "xa", "xp", "mdp", "ldp", "ndp", "mrg")]
+for _t in range(NF):
+    SEMAPHORES += ["fa%d" % _t, "fb%d" % _t]
+SEMAPHORES += ["ga%d" % _t for _t in range(len(WAY)) if WAY[_t] in "gG"]
 
-CY, GA, SC, PE = 0.9e-3, 1.5, 2.8, 0.43e-3
-WAKE, LAT = 0.05, 2.2
-LATE = 20.0
-LAND = {"arr": 3.0, "sar": 4.0, "brr": 4.0}
+CY, GA, SC, PE = 0.86e-3, 1.56, 3.5, 0.43e-3
+WAKE, LAT, TRIP, ADD = 0.05, 2.2, 10.5, 5.5
+XL = (6.0, 6.0, 7.5)
+ALL = (1 << 128) - 1
+BIG = 1.5 * 2 ** 27
+
+UNITS = []
+for _t in range(NR):
+    _e = [_i for _i in range(16) if _i != _t]
+    _k = 0
+    while _k < len(_e):
+        _n = 2 if (_t or _k) and _k + 1 < len(_e) and _e[_k + 1] == _e[_k] + 1 else 1
+        UNITS.append((_t, _e[_k], _n, sum(u[3] >= 0 for u in UNITS) if WAY[len(UNITS)] in "xX" else -1))
+        _k += _n
+UNITS.append(UNITS.pop(-7))
+
+
+def R(name, a=0, b=None, st=None, p=None):
+    return (name, a, SCRATCH[name][1][1] if b is None else b, st, p)
+
+
+def region(x):
+    if x[0].startswith("ps"):
+        return (x[0], x[1] // 512 * 512, (x[2] + 511) // 512 * 512, ALL)
+    if len(x) < 5 or x[4] is None:
+        return (x[0], x[1], x[2], ALL)
+    return (x[0], x[1], x[2], sum(1 << k for k in range(x[4][0], x[4][1], x[4][2] or 1)))
+
+
+def place(topo, c):
+    a = topo.addr(c)
+    return DstId(rid=a[0], pnc=a[1])
+
+
+def helper(topo, T, c):
+    return [k for k in topo.cores_of(c) if T.rank_of(k) is None and topo.die(k) == topo.die(c)][0]
+
+
+def hand_back(g, core, T, topo, home):
+    n = len(topo.engines(core, home))
+    for t, i, k, f in UNITS:
+        if f >= 0:
+            x = T.rb[:, 1024 * f:1024 * f + 512 * k]
+            g.wait_ge(T.sem["fa%d" % f], n)
+            g.remote_dma_fused([RemoteDMATransfer(dst_ids=[place(topo, home)], dma_engine_mask=topo.mask(core, home),
+                                                  remote_sem=T.sem["fb%d" % f], srcs=[x], dsts=[x])], local_sem=T.sem.loc)
+    g.wait_ge(T.sem.loc, n * NF)
 
 
 def rank_program(g, core, T, topo):
     r = T.rank_of(core)
     if r is None:
+        for c in T.cores:
+            if NF and helper(topo, T, c) == core:
+                hand_back(g, core, T, topo, c)
         return
     eng = {"v": g.vector, "a": g.scalar, "p": g.tensor, "g": g, "s": g.sync}
     tasks = []
     bonus, lift = {}, [0.0]
 
-    def op(e, fn, reads, writes, cost):
+    def add(e, kind, fn, sem, inc, reads, writes, busy, lat):
         bonus[len(tasks)] = lift[0]
-        tasks.append((e, "op", fn, "c" + e, 1, reads, writes, cost, cost))
+        tasks.append((e, kind, fn, sem, inc, [region(x) for x in reads], [region(x) for x in writes], busy, lat))
 
-    def dma(e, sem, out, in_, reads, writes, lat=LAT, first=0.0):
-        bonus[len(tasks)] = first
-        tasks.append((e, "dma", lambda q: q.dma_start(out, in_), sem, 16, reads, writes, 0.1, lat))
+    def turn(k):
+        lift[0] = -100.0 - k
 
-    def ap(rg):
-        return T[rg[0]][:, rg[1]:rg[2]]
+    def op(e, fn, reads, writes, cost):
+        add(e, "op", fn, "c" + e, 1, reads, writes, cost, cost)
 
-    def full(name):
-        return (name, 0, SCRATCH[name][1][1])
+    def dma(e, sem, out, in_, reads, writes, lat=LAT):
+        add(e, "dma", lambda q: q.dma_start(out, in_), sem, 16, reads, writes, 0.1, lat)
 
-    def blk(name, k, w=512):
-        return (name, w * k, w * k + w)
+    def ap(x):
+        p = x[4] or (0, 128, None)
+        return T[x[0]][p[0]:p[1]:p[2], x[1]:x[2]:x[3]]
 
-    def part(rg, q, n=4):
-        w = (rg[2] - rg[1]) // n
-        return (rg[0], rg[1] + q * w, rg[1] + q * w + w)
+    def blk(name, k, w=512, p=None):
+        return R(name, w * k, w * k + w, None, p)
 
-    def small(*rgs):
-        return all(SCRATCH[x[0]][0] == "sbuf" and SCRATCH[x[0]][2] in (BF, U2, F2) for x in rgs)
+    def col(name, k):
+        return R(name, k, k + 1)
+
+    def p32(b):
+        return (32 * b, 32 * b + 32, None)
+
+    def num(x):
+        return len(range(x[1], x[2], x[3] or 1))
+
+    def small(*xs):
+        return all(SCRATCH[x[0]][0] == "sbuf" and SCRATCH[x[0]][2] in (BF, U2, F2) for x in xs)
 
     def vc(n, f=1.0):
         return 0.02 + max(64, n * f) * CY
 
     def copy(e, out, in_):
-        n = in_[2] - in_[1]
         if e == "v":
-            op("v", lambda q: q.tensor_copy(ap(out), ap(in_)), [in_], [out], vc(n, 0.5 if small(out, in_) else 1))
+            op("v", lambda q: q.tensor_copy(ap(out), ap(in_)), [in_], [out], vc(num(in_), 0.5 if small(out, in_) else 1))
         else:
-            op("a", lambda q: q.activation(ap(out), ap(in_), AF.Copy), [in_], [out], 0.05 + n * CY)
+            act(out, in_, AF.Copy)
 
     def act(out, in_, func):
-        op("a", lambda q: q.activation(ap(out), ap(in_), func), [in_], [out], 0.05 + (in_[2] - in_[1]) * CY)
+        op("a", lambda q: q.activation(ap(out), ap(in_), func), [in_], [out], 0.05 + num(in_) * CY)
+
+    def times(out, in_, s, func=AF.Copy):
+        cols, f = ([s], ap(s)) if isinstance(s, tuple) else ([], s)
+        op("a", lambda q: q.activation(ap(out), ap(in_), func, scale=f), [in_] + cols, [out], 0.05 + num(in_) * CY)
 
     def tt(out, a, b, o):
         f = 1 if a[0].startswith("ps") or b[0].startswith("ps") else 2
-        op("v", lambda q: q.tensor_tensor(ap(out), ap(a), ap(b), o), [a, b], [out], vc(a[2] - a[1], f))
+        op("v", lambda q: q.tensor_tensor(ap(out), ap(a), ap(b), o), [a, b], [out], vc(num(a), f))
 
-    def ts(out, a, s1, o1):
-        op("v", lambda q: q.tensor_scalar(ap(out), ap(a), s1, None, o1), [a], [out], vc(a[2] - a[1], 0.5 if small(out, a) else 1))
+    def ts(out, a, s1, o1, s2=None, o2=None):
+        cols = [x for x in (s1, s2) if isinstance(x, tuple)]
+        s1, s2 = [ap(x) if isinstance(x, tuple) else x for x in (s1, s2)]
+        args = (s1, s2, o1) if o2 is None else (s1, s2, o1, o2)
+        op("v", lambda q: q.tensor_scalar(ap(out), ap(a), *args), [a] + cols, [out], vc(num(a), 0.5 if small(out, a) else 1))
 
     def gcost(off):
-        return 0.07 + 16 * (off[2] - off[1]) * GA * CY
+        return 0.07 + 16 * num(off) * GA * CY
 
-    def gather(e, out, win, off):
+    def gather(e, out, win, off, after=()):
         if e == "v":
-            op("v", lambda q: q.tensor_copy(ap(out), ap(win).indirect(ap(off))), [win, off], [out], gcost(off))
+            op("v", lambda q: q.tensor_copy(ap(out), ap(win).indirect(ap(off))), [win, off, *after], [out], gcost(off))
         else:
-            op("a", lambda q: q.activation(ap(out), ap(win).indirect(ap(off)), AF.Copy), [win, off], [out], gcost(off))
+            op("a", lambda q: q.activation(ap(out), ap(win).indirect(ap(off)), AF.Copy), [win, off, *after], [out], gcost(off))
 
-    def gather_less(out, win, off):
-        op("v", lambda q: q.tensor_scalar(ap(out), ap(win).indirect(ap(off)), -2048.0, None, OP.add), [win, off], [out], gcost(off))
+    def gather_op(out, win, off, other, o, done=()):
+        op("v", lambda q: q.tensor_tensor(ap(out), ap(win).indirect(ap(off)), ap(other), o), [win, off, other], [out, *done], gcost(off))
 
-    def mm(out, lhs, rhs, start, stop, bank=None):
-        op("p", lambda q: q.matmul(ap(out), ap(lhs), ap(rhs), start, stop), [lhs, rhs], [bank or out], 0.03 + (rhs[2] - rhs[1]) * PE)
+    def scatter(win, off, src):
+        op("v", lambda q: q.tensor_copy(ap(win).indirect(ap(off)), ap(src)), [off, src], [win], 0.07 + num(src) * SC * CY)
 
-    def gi(i):
-        return blk("gall", i, 128)
+    def mm(out, lhs, rhs, start=True, stop=True):
+        op("p", lambda q: q.matmul(ap(out), ap(lhs), ap(rhs), start, stop), [lhs, rhs], [out], 0.015 + max(64, num(rhs)) * PE)
 
-    def tj(t):
-        return blk("tj", t, 32)
+    def fill(x, val):
+        op("v", lambda q: q.memset(ap(x), val), [], [x], vc(num(x), 0.5))
 
-    def tl(t):
-        return blk("tl", t, 32)
+    def asel(out, in_, pat, cmp, base, cm, other=0.0):
+        op("g", lambda q: q.affine_select(ap(out), ap(in_), pat, cmp, other, base, cm), [in_], [out], 0.2 + 2 * CY * num(in_))
 
-    def li(t, i, n=1):
-        return ("li", 512 * t + 32 * i, 512 * t + 32 * i + 32 * n)
-
-    def li3(n, i, k=1):
-        return ("li", 1536 + 256 * n + 16 * i, 1536 + 256 * n + 16 * i + 16 * k)
-
-    def hw(t):
-        return blk("h", t, 4096)
-
-    def psz(w=512):
-        return ("psW", 512, 512 + w)
-
-    XW, AW = full("xs"), full("adjs")
-
-    dma("s", "ltv", T.tvs[:, :], T.tv[:, :], [], [full("tvs")], LAT, 1000.0)
-    dma("s", "ladj", T.adjs[:, :], T.adj[:, :], [], [full("adjs")], 7.0, 500.0)
-    dma("s", "lx", T.xs[:, 0:4096], T.x[:, :], [], [("xs", 0, 4096)], 10.0, 400.0)
-
-    def fill(rg, val, cost):
-        op("v", lambda q: q.memset(ap(rg), val), [], [rg], cost)
-
-    lift[0] = 200.0
-    fill(full("ones"), 1.0, 0.1)
-    lift[0] = 0.0
-    fill(full("bcb"), 1.0, 1.0)
-    fill(full("gall"), 0.0, 1.0)
-    fill(("xs", 4096, 4112), 0.0, 0.1)
-
-    def asel(out, in_, pat, cmp, base, cm):
-        op("g", lambda q: q.affine_select(ap(out), ap(in_), pat, cmp, 0.0, base, cm), [in_], [out], 0.2 + 2 * CY * (in_[2] - in_[1]))
-
-    one128 = full("ones")
-    lift[0] = 300.0
-    asel(full("c1"), ("ones", 0, 8), [[-16, 8]], OP.is_ge, 0, 1)
-    asel(full("c2"), full("c1"), [[16, 8]], OP.is_ge, 15, -1)
-    asel(full("im"), one128, [[-1, 128]], OP.is_equal, 0, 1)
-    half = [[0, 4], [-1, 2], [0, 16]]
-    asel(full("ev"), full("im"), half, OP.is_equal, 0, 0)
-    asel(full("od"), full("im"), half, OP.is_equal, 1, 0)
-    asel(full("dp"), one128, [[-1, 128]], OP.is_equal, -16, 1)
-    asel(full("dm"), one128, [[-1, 128]], OP.is_equal, 16, 1)
-    asel(full("de"), full("dp"), half, OP.is_equal, 0, 0)
-    asel(full("do"), full("dm"), half, OP.is_equal, 1, 0)
-    lift[0] = 250.0
-    asel(full("b1"), one128, [[-16, 8], [0, 16]], OP.is_ge, 0, 1)
-    asel(full("bm"), full("b1"), [[16, 8], [0, 16]], OP.is_ge, 15, -1)
-    asel(full("lt"), full("bm"), [[1, 128]], OP.is_gt, 0, -1)
-    lift[0] = 0.0
-    asel(full("bcb"), full("bcb"), [[-1, 16], [-16, 8], [0, 16]], OP.is_equal, 0, 1)
-
-    def zeros(s, *after):
-        op("g", lambda q: q.iota(ap(hw(s)), [[0, 4096]], 0, 0, allow_small_or_imprecise_dtypes=True), list(after), [hw(s)], 7.0)
-
-    for s in range(2):
-        zeros(s, full("lt"))
-
-    def diag(i):
-        op("v", lambda q: q.tensor_copy(T.gall[:, 128 * i + i:128 * i + 128:16], T.c2[:, :]), [full("c2")], [gi(i)], 0.12)
-
-    lift[0] = 200.0
-    copy("v", full("tvu"), full("tvs"))
-    for a, b in (("s00", "ev"), ("s11", "od"), ("s10", "de"), ("s01", "do")):
-        copy("v", full(a), full(b))
-    lift[0] = 0.0
-    for i in range(16):
-        diag(i)
-    for nm, f in (("hi", 0.5), ("nhi", -0.5), ("ni", -1.0), ("pi", 512.0), ("pn", -512.0), ("imf", 1.0), ("nif", -1.0)):
-        ts(full(nm), full("im"), f, OP.mult)
-    ts(full("gp"), ("gall", 0, 512), 64.0, OP.mult)
-    ts(full("gn"), ("gall", 0, 512), -64.0, OP.mult)
-
-    SEL = [["s00", "s01"], ["s10", "s11"]]
-
-    def flip(rows):
-        op("v", lambda q: q.transpose(T.ut[:, :], ap(rows)), [rows], [full("ut")], vc(256))
-
-    def pick(u, h):
-        op("p", lambda q: q.matmul(T.psX[:, 16 * u:16 * u + 16], T[SEL[u][h]][:, :], T.ut[:, 16 * h:512:32], h == 0, h == 1),
-           [full(SEL[u][h]), full("ut")], [("psX", 0, 32)], 0.06)
-
-    def ylist(u):
-        op("v", lambda q: q.tensor_scalar(T.tl[:, u:32:2], T.psX[:, 16 * u:16 * u + 16], 2048.0, None, OP.add),
-           [("psX", 0, 32)], [tl(0)], vc(16))
-
-    def ymix(u):
-        op("v", lambda q: q.tensor_copy(T.tj[:, u:32:2], T.tl[:, 16 * u:16 * u + 16]), [tl(0)], [tj(0)], vc(16))
-
-    def entry(i):
-        op("v", lambda q: q.tensor_scalar(ap(li(0, i)), T.psW[:, i:1024:32], 2048.0, None, OP.add), [full("psW")], [li(0, i)], vc(32))
-
-    def first_lists():
-        gather_less(blk("ce", 0), AW, blk("tvu", 0, 32))
-        flip(blk("ce", 0))
-        for u in range(2):
-            for h in range(2):
-                pick(u, h)
-        for u in range(2):
-            ylist(u)
-        for u in range(2):
-            ymix(u)
-        gather_less(full("cjf"), AW, tj(0))
-        flip(full("cjf"))
-        for u in range(2):
-            for h in range(2):
-                mm(("psW", 512 * u, 512 * u + 496), full(SEL[u][h]), ("ut", 16 * h, 16 * h + 496), h == 0, h == 1)
-        for i in range(1, 16):
-            entry(i)
-
-    def rows_v(t):
-        a, b = 512 * t, 32 * t
-        gather_less(blk("ce", t), AW, blk("tvu", t, 32))
-        for n in range(2):
-            dma("s", "stj%d" % t, T.zj[:, b + 16 * n:b + 16 * n + 16], T.ce[t::16, a + 256 * n:a + 256 * n + 256],
-                [blk("ce", t)], [("zj", b + 16 * n, b + 16 * n + 16)], LAT, 50.0)
-        for n in range(2):
-            dma("s", "stl%d" % t, T.zz[:, b + 16 * n:b + 16 * n + 16], T.ce[t + 16 * n::32, a:a + 512],
-                [blk("ce", t)], [("zz", b + 16 * n, b + 16 * n + 16)], LAT, 40.0)
-
-    def plus(out, a, b, step, src):
-        op("v", lambda q: q.tensor_scalar(T[out][:, a:b:step], ap(src), 2048.0, None, OP.add), [src], [(out, a, b)], vc(16))
-
-    def rows_y(t):
-        b = 32 * t
-        if t == 3:
-            plus("tj", b, b + 32, 1, ("zj", b, b + 32))
-        else:
-            for n in range(2):
-                plus("tj", b + n, b + 32, 2, ("zj", b + 16 * n, b + 16 * n + 16))
-        gather("v", blk("cj", t), AW, tj(t))
-        op("v", lambda q: q.transpose(T.tlf[:, b:b + 32], T.zz[:, b:b + 32]), [("zz", b, b + 32)], [("tlf", b, b + 32)], vc(32))
-        plus("tl", b, b + 32, 1, ("tlf", b, b + 32))
-        rest = [i for i in range(16) if i != t]
-        if t == 3:
-            for n in range(2):
-                for k, i in enumerate(rest):
-                    z = li3(n, i)
-                    dma("s", "sli3_%d" % ((15 * n + k) // 4), ap(z), T.cj[i::16, 1536 + 256 * n:1792 + 256 * n], [blk("cj", t)], [z],
-                        LAT + 0.12 * k)
-            return
-        for n, i in enumerate(rest):
-            dma("s", "sli%d_%d" % (t, n // 4), ap(li(t, i)), T.cj[i::16, 512 * t:512 * t + 512],
-                [blk("cj", t)], [li(t, i)], LAT + 0.12 * n)
-
-    lift[0] = 60.0
-    first_lists()
-    for fn in (rows_v, rows_y):
-        for t in range(1, NR):
-            lift[0] = 60.0 - 5 * t
-            fn(t)
-    lift[0] = 0.0
-
-    def prep(t):
-        b = t % 2
-        xv, xy, hb = blk("xv", b), blk("xy", b), blk("hh", b)
-        gather("a", xv, XW, blk("tvu", t, 32))
-        gather("a", xy, XW, tl(t))
-        mm(full("psX"), full("hi"), xv, True, False)
-        mm(full("psX"), full("hi"), xy, False, True)
-        if t == 3:
-            for n in range(2):
-                m1, m2 = ("m", 1024 + 512 * n, 1280 + 512 * n), ("m", 1280 + 512 * n, 1536 + 512 * n)
-                copy("a", m1, ("psX", 256 * n, 256 * n + 256))
-                dma("s", "mdp3", ap(m2), ap(m1), [m1], [m2], LAT + 0.3)
-        else:
-            m1, m2 = blk("m", 2 * b), blk("m", 2 * b + 1)
-            copy("a", m1, full("psX"))
-            if t:
-                dma("s", "mdp%d" % t, ap(m2), ap(m1), [m1], [m2], LAT + 0.6)
-            else:
-                copy("a", m2, full("psX"))
-        mm(full("psX"), full("hi"), xv, True, False)
-        mm(full("psX"), full("nhi"), xy, False, True)
-        act(hb, full("psX"), AF.Abs)
-
-    def mins(t):
-        n = NR if t == r else t + 1
-        yl = blk("yli", t, 32)
-        copy("v", yl, tl(t))
-        tt(blk("mini", 5 * t, 32), blk("tvs", t, 32), yl, OP.min)
-        if t == 3:
-            for k in range(2):
-                b = 384 + 64 * k
-                copy("v", ("lki", b, b + 48), li3(k, 0, 3))
-                for s in range(3):
-                    tt(part(blk("mini", 12 + s, 32), k, 2), ("lki", b + 16 * s, b + 16 * s + 16), part(yl, k, 2), OP.min)
-        else:
-            for a, b in ((0, t), (t + 1, n)):
-                if a < b:
-                    copy("v", ("lki", 128 * t + 32 * a, 128 * t + 32 * b), li(t, a, b - a))
-                for s in range(a, b):
-                    tt(blk("mini", 4 * t + s, 32), blk("lki", 4 * t + s, 32), yl, OP.min)
-        copy("v", ("mint", 128 * t, 128 * t + 32 * n), ("mini", 128 * t, 128 * t + 32 * n))
-
-    def cols(t):
-        zc, inv, eq, off = blk("zc", t), blk("inv", t), blk("eq", t), tl(t)
-        if t not in (r, 3):
-            zc, inv, off = part(zc, r), part(inv, r), part(off, r)
-        gather_less(zc, AW, off)
-        ts(inv, zc, 2048.0, OP.is_equal)
-        zq = blk("zc", t)
-        if t < 3:
-            zq, eq = part(zq, r), part(eq, r)
-        z = psz(zq[2] - zq[1])
-        mm(z, blk("bch", t, 128), zq, True, True)
-        tt(eq, z, zq, OP.is_equal)
-
-    def bigmats():
-        copy("v", full("bch"), full("bcb"))
-        ts(full("q16"), full("lt"), 16.0, OP.mult)
-        ts(full("nbm"), full("bm"), -1.0, OP.mult)
-        ts(full("b2k"), full("bm"), 2048.0, OP.mult)
-        tt(full("qm"), full("q16"), full("im"), OP.subtract)
-
-    units = []
-    for t in range(NR):
-        ent = [i for i in range(16) if i != t]
-        for c in range(2 if t == 3 else 1):
-            us = []
-            k = 0
-            while k < len(ent):
-                n = 2 if (t or k) and k + 1 < len(ent) and ent[k + 1] == ent[k] + 1 else 1
-                us.append((t, c, ent[k], n))
-                k += n
-            for j, u in enumerate(us):
-                units.append(u + (j == 0, j == len(us) - 1))
-    start = [[n for n, u in enumerate(units) if u[0] == t][0] for t in range(NR)] + [len(units)]
-
-    def unit(n):
-        t, ch, i, k, fst, lst = units[n]
-        wd = 256 if t == 3 else 512
-        c, d0, w0, p0, m0 = wd * k, 1024 * (n % ND), 1024 * (n % 3), 1024 * (n % 2), 1024 * (t % 2) + 512 * ch
-        d, w, s, m, off = ("d", d0, d0 + c), ("w", w0, w0 + c), ("s", w0, w0 + c), ("m", m0, m0 + c), li(t, i, k)
-        hq, acc = blk("hh", t % 2), full("psA")
-        if t == 3:
-            off = li3(ch, i, k)
-            hq = part(hq, ch, 2)
-            acc = ("psX" if ch else "psA", 0, 256)
-        op("v", lambda q: q.tensor_tensor(ap(d), ap(XW).indirect(ap(off)), ap(m), OP.subtract), [XW, off, m], [d], gcost(off))
-        act(w, d, AF.Abs)
-        for j in range(k):
-            o = ("psT", p0 + wd * j, p0 + wd * j + wd)
-            bank = ("psT", p0, p0 + 512) if t == 3 else o
-            mm(o, full("im"), ("w", w0 + wd * j, w0 + wd * j + wd), True, False, bank)
-            mm(o, full("ni"), hq, False, True, bank)
-        act(s, ("psT", p0, p0 + c), AF.Sign)
-        for j in range(k):
-            mm(acc, gi(i + j), ("s", w0 + wd * j, w0 + wd * j + wd), fst and j == 0, lst and j == k - 1)
-
-    others = [q for q in range(NR) if q != r]
-    links = topo.engines(core, T.cores[others[0]])
+    def token(name):
+        return ("token" + name, 0, 1)
 
     def dst(q):
-        a = topo.addr(T.cores[q])
-        return DstId(rid=a[0], pnc=a[1])
+        return place(topo, T.cores[q])
 
-    def remote(name, t, transfers, nloc, nrem, src, land):
-        tasks.append(("g", "send", lambda q: q.remote_dma_fused(transfers, local_sem=T.sem.loc), "loc", nloc, [src],
-                      [("token" + name, t, t + 1)], 0.6, 0.6))
-        tasks.append((None, "land", None, name + str(t), 3 * nrem, [("token" + name, t, t + 1)], land, 0.0, LAND[name]))
+    def some(engines):
+        return sum(1 << e for e in engines)
 
-    def share(t):
-        mine = blk("part", t)
-        copy("a", mine, full("psA"))
-        k = len(links) // 4
-        tr = []
-        for n, q in enumerate(others):
-            mask = sum(1 << e for e in links[n * k:n * k + k])
-            tr.append(RemoteDMATransfer(dst_ids=[dst(q)], dma_engine_mask=mask, remote_sem=T.sem["arr%d" % t],
-                                        srcs=[ap(part(mine, q))], dsts=[ap(part(blk("pin", t), r))]))
-        remote("arr", t, tr, 3 * k, k, mine, [part(blk("pin", t), q) for q in others])
+    def remote(name, transfers, nloc, nrem, srcs, land, lat):
+        add("g", "send", lambda q: q.remote_dma_fused(transfers, local_sem=T.sem.loc), "loc", nloc, srcs, [token(name)], 0.6, 0.6)
+        add(None, "land", None, name, nrem, [token(name)] + srcs, land, 0.0, lat)
 
-    def pin3(q, a, b):
-        return ("pin", 1536 + 512 * q + a, 1536 + 512 * q + b)
+    XW, AW, MK, TB = R("xs"), R("adjw"), R("mk"), R("tb")
+    PW, PF = R("psW"), R("psF")
+    others = [(r + 1 + k) % NR for k in range(NR - 1)]
+    links = topo.engines(core, T.cores[others[0]])
+    wide = topo.mask(core, T.cores[others[0]])
+    mate = helper(topo, T, core)
+    near = topo.engines(core, mate)
+    own = slice(32 * r, 32 * r + 32)
 
-    def share_all(ch):
-        a = 256 * ch
-        mine = ("part", 1536 + a, 1792 + a)
-        copy("a", mine, ("psX" if ch else "psA", 0, 256))
-        name = "brr" if ch else "arr"
-        tr = [RemoteDMATransfer(dst_ids=[dst(q) for q in others], dma_engine_mask=topo.mask(core, T.cores[others[0]]),
-                                remote_sem=T.sem[name + "3"], srcs=[ap(mine)], dsts=[ap(pin3(r, a, a + 256)) for _ in others])]
-        remote(name, 3, tr, len(links), len(links), mine, [pin3(q, a, a + 256) for q in others])
+    def stage(k, lat):
+        q = others[k]
+        dma("s", "lx%d" % k, ap(blk("xst", k, 1024)), T.x[32 * q:32 * q + 32, :], [], [blk("xst", k, 1024)], lat)
 
-    def rk(t, s):
-        return blk("rk", 4 * t + s)
-
-    def mi(t, s):
-        return blk("mint", 4 * t + s, 32)
-
-    def look(t, s):
-        if t in (r, 3):
-            gather("a", rk(t, s), hw(s), mi(t, s))
-        else:
-            gather("a", part(rk(t, s), r), hw(s), part(mi(t, s), r))
-
-    def decide(t, a, b):
-        def cut(rg):
-            return (rg[0], rg[1] + a, rg[1] + b)
-        w = b - a
-        X, W, K, FI, FZ = [(nm, 0, w) for nm in ("psW", "wsum", "ok", "first", "fz")]
-        mm(X, full("pi"), cut(blk("eq", t)), True, False)
-        mm(X, full("pi"), cut(blk("inv", t)), False, False)
-        for s in range(t):
-            mm(X, blk("gp", s, 128), cut(rk(t, s)), False, False)
-        mm(X, full("im"), cut(blk("part", t)), False, False)
-        for q in others:
-            mm(X, full("im"), pin3(q, a, b) if t == 3 else part(blk("pin", t), q), False, q == others[-1])
-        act(W, X, AF.Abs)
-        ts(K, W, 8.0, OP.is_le)
-        mm(X, full("qm"), K, True, True)
-        ts(FI, X, -1.0, OP.is_equal)
-        tt(FZ, FI, cut(blk("zc", t)), OP.mult)
-        mm(X, full("b2k"), FI, True, False)
-        mm(X, full("nbm"), FZ, False, True)
-        mine = cut(blk("sepin", t))
-        copy("v", mine, X)
-        if t == 3:
-            return
-        tr = [RemoteDMATransfer(dst_ids=[dst(q) for q in others], dma_engine_mask=topo.mask(core, T.cores[others[0]]),
-                                remote_sem=T.sem["sar%d" % t], srcs=[ap(mine)], dsts=[ap(mine) for _ in others])]
-        remote("sar", t, tr, len(links), len(links), mine, [part(blk("sepin", t), q) for q in others])
-
-    def mark(t, a, b):
-        if t == 3 and r == 3:
-            return
-        off, src = ("mint", 160 * t + a // 16, 160 * t + b // 16), ("sepin", 512 * t + a, 512 * t + b)
-        op("v", lambda q: q.tensor_copy(ap(hw(t)).indirect(ap(off)), ap(src)), [off, src], [hw(t)], 0.07 + (b - a) * SC * CY)
-
-    def seps(t, a, b):
-        a, b = 512 * t + a, 512 * t + b
-        out, src = ("sepf", a, b), ("sepin", a, b)
-        op("v", lambda q: q.tensor_scalar(ap(out), ap(src), -1.0, 4096.0, OP.mult, OP.add), [src], [out], vc(b - a))
-        dma("s", "osep%d" % t, T.ysep[:, a:b], T.sepf[0::16, a:b], [out], [])
-
-    def mj(j):
-        return blk("mt_", j)
-
-    def fl_lists():
-        for n in range(2):
-            dma("s", "svj", T.zv[:, 16 * n:16 * n + 16], T.zc[r::16, 512 * r + 256 * n:512 * r + 256 * n + 256],
-                [blk("zc", r)], [("zv", 16 * n, 16 * n + 16)])
-        for n in range(2):
-            plus("vj", n, 32, 2, ("zv", 16 * n, 16 * n + 16))
-        gather("v", full("cvj"), AW, full("vj"))
-        for s in range(NR):
-            dma("s", "slv", ap(blk("lv", s, 32)), T.cvj[s::16, :], [full("cvj")], [blk("lv", s, 32)])
-        copy("v", full("lvi"), full("lv"))
-        for s in range(NR):
-            if s != r:
-                tt(blk("mvi", s, 32), blk("lvi", s, 32), blk("tvs", r, 32), OP.min)
-        for a, b in ((0, r), (r + 1, NR)):
-            if a < b:
-                copy("v", ("mv", 32 * a, 32 * b), ("mvi", 32 * a, 32 * b))
-
-    def match(j):
-        mm(psz(), blk("bch", j, 128), blk("ce", r), True, True)
-        tt(mj(j), psz(), blk("zc", r), OP.is_equal)
-
-    def fl_own(a, b):
-        src, sf, z = ("sepin", 512 * r + a, 512 * r + b), ("sf", a, b), psz(b - a)
-        op("v", lambda q: q.tensor_scalar(ap(sf), ap(src), -1.0, 2048.0, OP.mult, OP.add), [src], [sf], vc((b - a) / 2))
-        mm(z, full("imf"), sf, True, False)
-        mm(z, full("nif"), ("zc", 512 * r + a, 512 * r + b), False, True)
-        ts(("eqs", a, b), z, 0.0, OP.is_equal)
-        ts(("nh", a, b), src, 0.0, OP.is_equal)
-
-    def fl_gather(s):
-        if s != r:
-            gather("v", blk("rv", s), hw(s), blk("mv", s, 32))
-            if s > r:
-                look(r, s)
-
-    def fl_round(s):
-        if s != r:
-            mm(psz(), full("im"), mj(s), True, s == 3)
-            if s == 3:
-                tt(blk("mg", s), psz(), blk("rv", s), OP.is_gt)
-            else:
-                mm(psz(), full("ni"), blk("rv", s), False, True)
-                act(blk("mg", s), psz(), AF.Relu)
-            mm(F, full("im"), blk("mg", s), False, s == 3)
-            if s != 3:
-                mm(F, blk("gn", s, 128), rk(r, s), False, False)
-
-    F = full("psA")
-    mine = (128 * r, 128 * r + 128)
+    lift[0] = 1000.0
+    stage(0, 3.0)
+    lift[0] = 800.0
+    for b in range(4):
+        x = R("adjq", p=p32(b))
+        dma("a", "ladj", ap(x), T.adj[own, 1024 * b:1024 * b + 1024], [], [x], 4.2)
+    lift[0] = 750.0
     for t in range(NR):
-        lift[0] = 20.0 if t else 60.0
-        prep(t)
-        lift[0] = 0.0
+        for c in range(4):
+            x = blk("tvs", t, 8, p32(c))
+            dma("sa"[t % 2], "ltv", ap(x), T.tv[own, 32 * t + 8 * c:32 * t + 8 * c + 8], [], [x], 4.0)
+    lift[0] = 700.0
+    stage(1, 4.4)
+    stage(2, 5.1)
+    lift[0] = 2000.0
+    for k, q in enumerate(others):
+        tr = [RemoteDMATransfer(dst_ids=[dst(q)], dma_engine_mask=wide, remote_sem=T.sem["xa%d" % k],
+                                srcs=[ap(blk("xst", k, 1024))], dsts=[ap(blk("xin", k, 1024))])]
+        remote("xa%d" % k, tr, len(links), len(links), [blk("xst", k, 1024)], [blk("xin", k, 1024)], XL[k])
+    x = R("xs", 0, 4096, p=p32(r))
+    dma("s", "lown", ap(x), T.x[own, :], [blk("xin", 0, 1024)], [x], 3.5)
+    for k in range(NR - 1):
+        x = R("xs", 0, 4096, p=p32((r - 1 - k) % NR))
+        dma("s", "xp%d" % k, ap(x), ap(blk("xin", k, 1024)), [blk("xin", k, 1024)], [x], 3.0)
+
+    one = R("ones")
+    lift[0] = 600.0
+    fill(one, 1.0)
+    asel(R("a0"), one, [[0, 4], [-1, 32]], OP.is_equal, 0, 1)
+    asel(R("a1"), one, [[0, 4], [-1, 32]], OP.is_equal, 16, 1)
+    lift[0] = 500.0
+    asel(R("pm"), one, [[-16, 2], [-1, 16], [-32, 4]], OP.is_equal, 0, 1)
+    asel(R("im"), one, [[-1, 128]], OP.is_equal, 0, 1)
+    asel(R("b1"), one, [[-16, 8], [0, 16]], OP.is_ge, 0, 1)
+    asel(R("bm"), R("b1"), [[16, 8], [0, 16]], OP.is_ge, 15, -1)
+    p16 = (0, 16, None)
+    half = [R("a0", p=p16), R("a1", p=p16)]
+    lift[0] = 600.0
+    mm(blk("psF", 0, 128), R("a0", p=p32(0)), R("a0", p=p32(0)))
+    copy("v", R("r32"), blk("psF", 0, 128))
+    for u in range(2):
+        for a in range(2):
+            mm(blk("psW", 2 * u + a, 128), half[u], half[a])
+    lift[0] = 400.0
+    fill(R("bc"), 0.0)
+    for b in range(4):
+        fill(R("bc", b, b + 1, p=p32(b)), 1.0)
+        fill(R("bc", 4 + b, 5 + b, p=p32(b)), 32.0)
+    for b in range(4):
+        ts(blk("sel", b), PW, col("bc", b), OP.mult)
+    for a in range(2):
+        mm(R("psA", 0, 16), half[a], R("im", 0, 16, p=p16), a == 0, a == 1)
+    for a in range(2):
+        mm(R("psA", 16 + a, 17 + a), half[a], R("ones", 0, 1, p=p16))
+    fill(R("gs"), 0.0)
+    copy("a", R("r16"), R("psA", 0, 16))
+    copy("a", R("gs", 111, 128, 16), R("psA", 16, 18))
+    for nm, f in (("ni", -1.0), ("hi", 0.5), ("nhi", -0.5), ("pi", 512.0), ("n2", -2.0)):
+        times(R(nm), R("im"), f)
+    lift[0] = 300.0
+    for j in range(16):
+        if j % 2:
+            times(blk("bch", j, 128), R("bm"), col("r16", j))
+        else:
+            ts(blk("bch", j, 128), R("bm"), col("r16", j), OP.mult)
+    fill(R("xs", 4096, 4112), 0.0)
+    fill(R("bz"), 0.0)
+    fill(R("hw"), 0.0)
+    lift[0] = 500.0
+    copy("v", R("tvd"), R("tvs"))
+
+    lift[0] = 0.0
+    asel(R("lt"), R("bm"), [[1, 128]], OP.is_gt, 0, -1)
+    asel(R("k1"), R("bm"), [[-16, 8], [-4, 16]], OP.is_ge, 0, 1)
+    asel(R("km"), R("k1"), [[16, 8], [4, 16]], OP.is_ge, 3, -1)
+    asel(R("z1"), one, [[-16, 2], [-32, 16], [-1000, 4]], OP.is_ge, 0, 1)
+    asel(R("bz", 51, 179), R("z1"), [[16, 2], [32, 16], [1000, 4]], OP.is_ge, 15, -1)
+    asel(R("g1"), one, [[-16, 2], [0, 16], [-32, 4]], OP.is_ge, 0, 1)
+    asel(R("gm"), R("g1"), [[16, 2], [0, 16], [32, 4]], OP.is_ge, 15, -1)
+    asel(R("l1"), R("gm"), [[-16, 2], [-4, 16], [-32, 4]], OP.is_ge, 0, 1)
+    asel(R("lm"), R("l1"), [[16, 2], [4, 16], [32, 4]], OP.is_ge, 3, -1)
+    asel(R("v2"), one, [[0, 4], [-1, 2], [0, 16]], OP.is_equal, 0, 1)
+    times(R("q16"), R("lt"), 16.0)
+    asel(R("qm"), R("q16"), [[-1, 128]], OP.not_equal, 0, 1, -1.0)
+
+    def iota(x, step, base, after, cost):
+        op("g", lambda q: q.iota(ap(x), [[step, num(x)]], base, 0, allow_small_or_imprecise_dtypes=True), after, [x], cost)
+
+    places = ((1, 1), (129, 1), (258, 2), (516, 4))
+    for c, (base, step) in enumerate(places):
+        iota(R("ix", p=p32(c)), step, base, [token("xa2")], 0.4)
+    iota(MK, 0, 0, [token("xa2"), R("lm"), R("km"), R("bz"), R("qm"), R("v2"), R("ix")], 7.0)
+    dma("s", "ltb", ap(TB), ap(MK), [MK, XW], [TB], 5.0)
+
+    lift[0] = 450.0
+    banks = [blk("psT", k) for k in range(4)] + [blk("psA", 0), blk("psA", 1), PF, PW]
+    for h in range(2):
+        ts(blk("adjh", h), blk("adjq", h), -2048.0, OP.add)
+        for b in range(4):
+            mm(banks[4 * h + b], R("r32", p=p32(b)), blk("adjh", h, 512, p32(b)))
+    for h in range(2):
+        for b in range(4):
+            copy("v" if 4 * h + b in (3, 5, 7) else "a", blk("adjw", 2 * b + h), banks[4 * h + b])
+
+    def spread(bank, n, rows, c0):
+        for w in range(8):
+            for a in range(2):
+                mm(R(bank[0], bank[1] + w, bank[1] + 8 * n, 8), blk("sel", 2 * w + a, 128),
+                   R(rows, c0 + n * a, c0 + n * a + n), a == 0, a == 1)
+
+    def li(t, i, n=1):
+        return R("li", 512 * t + 32 * i, 512 * t + 32 * i + 32 * n)
+
+    gather("v", R("cv"), AW, R("tvd"))
+    for t in range(NR):
+        for a in range(2):
+            mm(R("psW", 16 * a + t, 16 * a + 16, 4), blk("cv", t, 128), R("pm", 64 * a + 4 * t, 64 * a + 4 * t + 4))
+    copy("v", R("ty", 0, 32), R("psW", 0, 32))
+    spread(PF, 16, "ty", 0)
+    for c in range(4):
+        ts(R("yd", p=p32(c)), blk("psF", c, 32, p32(c)), 2048.0, OP.add)
+    gather("v", R("cy"), AW, R("yd"))
+    lift[0] = 250.0
+    for t in range(NR):
+        for a in range(2):
+            mm(R("psT", 16 * a + 4 * t, 16 * a + 4 * t + 4), blk("cv", t, 128), R("pm", 64 * a + 4 * t, 64 * a + 4 * t + 4))
+    copy("v", R("ty", 32, 64), R("psT", 0, 32))
+    spread(blk("psA", 0), 16, "ty", 32)
+    ts(R("yx"), R("psA", 0, 128), 2048.0, OP.add)
+    lift[0] = 270.0
+    for t in range(NR):
+        mm(blk("psW", t, 128), blk("cy", t, 128), R("pm"))
+    copy("v", R("tz"), PW)
+    def lists(t, bank):
+        spread(bank, 64, "tz", 128 * t)
+        ts(li(t, 0, 16), bank, 2048.0, OP.add)
+
+    for t in range(NR - 1):
+        lift[0] = (270.0, 230.0, 220.0)[t]
+        lists(t, (blk("psT", 0), PF, blk("psA", 0))[t])
         if t == 0:
-            bigmats()
-            cols(r)
+            lift[0] = 250.0
             for k in range(NR):
-                mins(k)
-                if k != r:
-                    cols(k)
-        for n in range(start[t + 1] - start[t]):
-            unit(start[t] + n)
-            if t and n == 2:
-                for s in range(t - 1):
-                    look(t, s)
-                decide(t - 1, *mine)
-            if t and n == 5:
-                mark(t - 1, 0, 512)
-                look(t, t - 1)
-                seps(t - 1, 0, 512)
-                fl_gather(t - 1)
-            if units[start[t] + n][5] and t == 3:
-                share_all(units[start[t] + n][1])
-        if t == 0:
-            fl_lists()
-            lift[0] = LATE
-            for j in range(16):
-                if j != r:
-                    match(j)
-            lift[0] = 0.0
+                mm(blk("psW", k, 128), blk("bch", k, 128), blk("cy", k, 128))
+            tt(R("eq"), PW, R("cy"), OP.is_equal)
+            ts(R("inv"), R("cy"), 2048.0, OP.is_equal)
+
+    def match(j, bank):
+        if MATCH[j] == "a":
+            mm(bank, blk("bch", j, 128), R("cv"), True, False)
+            mm(bank, R("ni"), R("cy"), False, True)
+            copy("a", blk("mt", j), bank)
+            if j < NE:
+                turn(2 + j)
+            ts(blk("mt", j), blk("mt", j), 0.0, OP.is_equal)
+        else:
+            mm(bank, blk("bch", j, 128), R("cv"))
+            tt(blk("mt", j), bank, R("cy"), OP.is_equal)
+
+    for j in range(NE):
+        lift[0] = 260.0
+        match(j, (blk("psA", 1), blk("psT", 1), blk("psT", 2))[j % 3])
+
+    def late_constants():
+        lift[0] = 100.0
+        mm(R("psT", 1536, 1540), half[0], R("km", 0, 4, p=p16), True, False)
+        mm(R("psT", 1536, 1540), half[1], R("km", 0, 4, p=p16), False, True)
+        mm(R("psT", 1664, 1792), R("v2", p=p16), R("v2", p=p16))
+        copy("a", R("rowm", 0, 4), R("psT", 1536, 1540))
+        for c in range(4):
+            times(blk("sb", c, 128), R("psT", 1664, 1792), col("bc", c))
+        turn(4)
+        last = col("rowm", 3)
+        ts(col("rowm", 4), last, -512.0, OP.mult, 512.0, OP.add)
+        ts(col("rowm", 5), last, 512.0, OP.mult, -512.0, OP.add)
+        ts(col("rowm", 6), col("r16", 3), -512.0, OP.mult)
+        for nm, src, f in (("pn", "pm", -512.0), ("gp", "gm", 128.0), ("nbz", "bz", -2048.0), ("gs2", "gs", 2.0), ("lk", "km", col("rowm", 4)),
+                           ("lpn", "lm", col("rowm", 5)), ("pn3", "pm", col("rowm", 6)), ("ixs", "ix", last)):
+            times(R(nm), R(src), f)
+        for c in range(4):
+            times(blk("gq", c, 128), R("gm"), col("bc", 4 + c))
+        for s in range(NR - 1):
+            times(blk("bs", s, 128), R("bm"), col("rowm", s))
+        for a in range(2):
+            times(blk("w1", a, 4), R("gm", 64 * a, 64 * a + 4), last)
+        mark(3, R("ixs"))
+
+    def mark(t, src):
+        scatter(MK, blk("tvd", t, 8), src)
+        scatter(MK, blk("yd", t, 8), src)
+        for a in range(2):
+            for c in range(4):
+                z = 16 * a + 4 * t
+                out, rows = R("tb", p=(z + c, 128, 32)), R("mk", p=(32 * c + z, 32 * c + z + 4, None))
+                dma("s", "mrg%d" % t, ap(out), ap(rows), [rows], [out], LAT + 0.6)
+
+    def prep(t, after=()):
+        b = t % 2
+        xv, xy, hb = blk("xv", b), blk("xy", b), blk("hh", t)
+        m1, m2, l1, l2 = blk("m", 2 * b), blk("m", 2 * b + 1), blk("lo", 2 * b), blk("lo", 2 * b + 1)
+        ph = PW if t else blk("psT", 3)
+        ways = WAY[8 * t:8 * t + 8]
+        if t:
+            gather(PREP[0], xv, XW, li(t, t), after)
+            gather(PREP[1], xy, XW, blk("yx", t, 32), after)
+            mm(PW, R("hi"), xv, True, False)
+            mm(PW, R("hi"), xy, False, True)
+            copy(PREP[2], m1, PW)
+            dma("s", "mdp%d" % t, ap(m2), ap(m1), [m1], [m2], LAT + 0.6)
+        else:
+            for h, bank in enumerate((R("psW", 0, 256), R("psA", 512, 768))):
+                gather("a", blk("xv", h, 256), XW, blk("li", h, 16))
+                gather("v", blk("xy", h, 256), XW, blk("yx", h, 16))
+                mm(bank, R("hi"), blk("xv", h, 256), True, False)
+                mm(bank, R("hi"), blk("xy", h, 256), False, True)
+                copy("av"[h], blk("m", h, 256), bank)
+            dma("s", "mdp0", ap(m2), ap(m1), [m1], [m2], LAT + 0.6)
+        mm(ph, R("hi"), xv, True, False)
+        mm(ph, R("nhi"), xy, False, True)
+        act(hb, ph, AF.Abs)
+        if "g" in ways.lower():
+            n1, n2 = blk("nh", 2 * b), blk("nh", 2 * b + 1)
+            if NEG == "v":
+                ts(n1, hb, -1.0, OP.mult)
+            else:
+                times(n1, hb, -1.0)
+            dma("s", "ndp%d" % t, ap(n2), ap(n1), [n1], [n2], LAT + 0.3)
+        if "x" in ways.lower():
+            mm(PW, R("hi"), xv, True, False)
+            mm(PW, R("hi"), xy, False, False)
+            mm(PW, R("ni"), hb, False, True)
+            copy("a", l1, PW)
+            dma("s", "ldp%d" % t, ap(l2), ap(l1), [l1], [l2], LAT + 0.3)
+
+    def acc(t, k=0):
+        return R("psA", 512 * (t % 2) + 128 * k, 512 * (t % 2) + 128 * k + 128)
+
+    def slot(name, n, k):
+        return R(name, 1024 * n, 1024 * n + 512 * k)
+
+    def part(x, j):
+        return R(x[0], x[1] + 512 * j, x[1] + 512 * j + 512)
+
+    def produce(n):
+        t, i, k, f = UNITS[n]
+        d = slot("d", n % ND, k)
+        turn(n - 2)
+        if n == 1:
+            for j in range(k):
+                gather_op(part(d, j), XW, li(t, i + j), slot("m", 0, 1), OP.subtract)
+        else:
+            gather_op(d, XW, li(t, i, k), slot("m" if f < 0 else "lo", t % 2, k), OP.subtract, [token("u%d" % n)])
+        if f >= 0:
+            e = len(near) // k
+            tr = [RemoteDMATransfer(dst_ids=[place(topo, mate)], dma_engine_mask=some(near[j * e:j * e + e]), remote_sem=T.sem["fa%d" % f],
+                                    srcs=[ap(part(d, j)), ap(blk("hh", t))], dsts=[ap(part(slot("rb", f, k), j))], alu_op=3)
+                  for j in range(k)]
+            remote("fb%d" % f, tr, len(near), len(near), [d, blk("hh", t)], [slot("rb", f, k)], TRIP)
+
+    used, size = {"w": 0, "psT": 0}, {}
+
+    def absolute(n):
+        t, i, k, f = UNITS[n]
+        w = size[n] = slot("w", used["w"] % NW, k)
+        used["w"] += 1
+        turn(n)
+        act(w, slot("d", n % ND, k), AF.Abs)
+        if WAY[n] in "gG":
+            nh = slot("nh", t % 2, k)
+            add("g", "dma", lambda q: q.dma_start(ap(w), ap(nh), accum_op=OP.add), "ga%d" % n, 16, [w, nh], [w], 1.0, ADD)
+
+    def consume(n, c, lst):
+        t, i, k, f = UNITS[n]
+        d, s = slot("d", n % ND, k), slot("s", c % 3, k)
+        if WAY[n] in "gG":
+            u = size[n]
+        else:
+            u = slot("psT", used["psT"] % 2, k)
+            used["psT"] += 1
+            turn(c + 1)
+            for j in range(k):
+                if f < 0:
+                    mm(part(u, j), R("ni"), blk("hh", t), True, False)
+                    mm(part(u, j), R("im"), part(size[n], j), False, True)
+                else:
+                    mm(part(u, j), R("im"), part(d, j), True, False)
+                    mm(part(u, j), R("n2"), part(slot("rb", f, k), j), False, True)
+        turn(c + 1.5)
+        vec = WAY[n] in ":XG"
+        if vec:
+            ts(s, u, -0.5, OP.max, 0.5, OP.min)
+        else:
+            act(s, u, AF.Sign)
+        turn(c + 2.2)
+        for j in range(k):
+            for b in range(4):
+                z, a = 111 - 32 * b - i - j, s[1] + 512 * j + 128 * b
+                mm(acc(t), R("gs2" if vec else "gs", z, z + 128), R("s", a, a + 128), False, lst and j == k - 1 and b == 3)
+
+    def passed(t):
+        mm(acc(t), R("pi"), blk("eq", t, 128), True, False)
+        mm(acc(t), R("pi"), blk("inv", t, 128), False, False)
+
+    def look(t):
+        gather("a", blk("rk", t, 128), TB, blk("yd", t, 8))
+        mm(acc(t), R("lk"), blk("rk", t, 128), False, False)
+
+    def decide(t):
+        K, FI, FZ, CY_ = R("ok"), blk("fi", t, 128), blk("fz", t, 128), blk("cy", t, 128)
+        ts(K, acc(t), BIG, OP.add, BIG, OP.is_equal)
         if t < 3:
-            share(t)
-        if t == 0:
-            for s in range(2, NR if r != 3 else 3):
-                zeros(s, ("tokenarr", 0, 1))
-    mm(F, full("pn"), blk("inv", r), True, False)
-    for j in range(4, 16):
-        mm(F, full("im"), mj(j), False, False)
-    for s in range(3):
-        if s != r:
-            fl_round(s)
-    if r != 3:
-        fl_own(0, 512)
-        mm(F, full("pn"), full("eqs"), False, False)
-        mm(F, full("pn"), full("nh"), False, False)
-    for c in range(2):
-        a, b = 256 * c, 256 * c + 256
-        decide(3, a, b)
-        mark(3, a, b)
-        seps(3, a, b)
-        if r == 3:
-            fl_own(a, b)
-    if r != 3:
-        fl_gather(3)
-        mm(F, blk("gn", 3, 128), rk(r, 3), False, False)
-        fl_round(3)
-    else:
-        mm(F, full("pn"), full("nh"), False, False)
-        mm(F, full("pn"), full("eqs"), False, True)
-    ts(full("fl"), F, 0.0, OP.is_gt)
-    dma("s", "oflag", T.yflag[:, :], T.fl[:, :], [full("fl")], [])
+            HS = blk("hs", t, 128)
+            mm(acc(t, 1), R("bm"), K)
+            mm(acc(t, 2), R("qm"), K)
+            ts(HS, acc(t, 1), 0.0, OP.is_gt, col("rowm", t), OP.mult)
+            ts(FI, acc(t, 2), -1.0, OP.is_equal)
+            mark(t, HS)
+        else:
+            for c in (2, 3, 0, 1):
+                mm(blk("psA" if c else "psT", c, 128), blk("sb", c, 128), K)
+            mm(acc(t, 2), R("qm"), K)
+            for c, (base, step) in enumerate(places):
+                if c:
+                    act(R("hw", base, base + 128 * step, step), blk("psA", c, 128), AF.Sign)
+                else:
+                    ts(R("hw", base, base + 128), blk("psT", 0, 128), 0.0, OP.is_gt)
+            ts(FI, acc(t, 2), -1.0, OP.is_equal)
+        tt(FZ, FI, CY_, OP.mult)
+        mm(acc(t, 3), R("bm"), FZ)
+        tt(blk("eqs", t, 128), acc(t, 3), CY_, OP.is_equal)
+
+    def seps(t):
+        for x in range(4):
+            z, a = 51 - 16 * t - x, 128 * t + 32 * x
+            mm(R("psW", 0, 32), R("bz", z, z + 128), R("fz", a, a + 32), t == 0 and x == 0, False)
+            mm(R("psW", 0, 32), R("nbz", z, z + 128), R("fi", a, a + 32), False, t == 3 and x == 3)
+
+    def live(s, bank):
+        if LIVE[s] == "v":
+            mm(bank, blk("bs", s, 128), R("rv"))
+            tt(blk("mg", s), bank, blk("mt", s), OP.is_lt)
+        else:
+            mm(bank, blk("bs", s, 128), R("rv"), True, False)
+            mm(bank, R("ni"), blk("mt", s), False, True)
+            times(blk("mg", s), bank, -1.0, AF.Relu)
+
+    def flag(lhs, src, a, b, c0=0, start=False, stop=False):
+        mm(R("psF", a, b), R(lhs), R(src, c0 + a, c0 + b), start, stop)
+
+    def after_two(c):
+        gather("a", R("rv"), TB, R("tvd"))
+        gather("a", blk("rk", 0, 128), TB, blk("yd", 0, 8))
+        for k in range(6):
+            for a in range(2):
+                mm(R("psW", 24 * a + k, 24 * a + 24, 6), blk("rv" if k > 2 else "rk", k % 3, 128), blk("w1", a, 4))
+        copy("v", R("tx"), R("psW", 0, 48))
+        spread(PW, 24, "tx", 0)
+        for b in range(4):
+            copy("v", R("xl", p=p32(b)), blk("psW", b, 48, p32(b)))
+        for s in range(2):
+            turn(c + 1 + s)
+            live(s, PW)
+            flag("pm", "mg", 0, 512, 512 * s)
+
+    def after_three():
+        gather("a", R("rv"), TB, R("tvd"))
+        gather("v", R("ry"), TB, R("yd", 0, 16))
+        flag("gp", "hs", 0, 384)
+        flag("pn", "eqs", 0, 384)
+        flag("lpn", "rk", 256, 512)
+        flag("lpn", "ry", 0, 256)
+        live(2, blk("psA", 0))
+        flag("pm", "mg", 0, 512, 1024)
+
+    late_constants()
+    lift[0] = 500.0
+    prep(0)
+    order = sorted(range(len(UNITS)), key=lambda n: n + LAG[WAY[n]])
+    made, seen = 0, []
+    for c, n in enumerate(order):
+        while made < len(UNITS) and (made <= n or made <= c + 2) and (made < ND or made - ND in seen):
+            t = UNITS[made][0]
+            k = made - [u[0] for u in UNITS].index(t)
+            if k == 3 and t < 3:
+                turn(made)
+                prep(t + 1, [token("u%d" % (made - 1))])
+            produce(made)
+            made += 1
+        for z in range(made):
+            if WAY[z] not in "xX" and z not in size and (z <= n + LAG[WAY[n]] + 1):
+                absolute(z)
+        t = UNITS[n][0]
+        mine = [z for z in order if UNITS[z][0] == t]
+        if n == mine[0]:
+            turn(c)
+            passed(t)
+        if c == 1:
+            for j in range(NE, 16):
+                turn(MK0 + MK1 * (j - NE))
+                match(j, PF)
+        if c == 12:
+            turn(c)
+            lists(3, PF)
+            for j in range(4, 16):
+                turn(c + (j - 4) / 3)
+                flag("pm", "mt", 0, 512, 512 * j, j == 4)
+            flag("pn", "inv", 0, 512)
+        if n == mine[-1] and t:
+            turn(c - 4)
+            look(t)
+            if t == 2:
+                after_two(c - 2)
+            if t == 3:
+                for s in range(3):
+                    seps(s)
+                after_three()
+        consume(n, c, n == mine[-1])
+        seen.append(n)
+        if n == mine[-1]:
+            turn(c - 1)
+            decide(t)
+    turn(len(UNITS) + 2)
+    HW = R("hw")
+    gather("a", R("ru"), HW, R("xl", 0, 24))
+    gather_op(R("mg", 1536, 1920), HW, R("xl", 24, 48), R("mt", 1536, 1920), OP.is_lt)
+    for c, (base, step) in enumerate(places):
+        mm(R("psF", 384, 512), blk("gq", c, 128), R("hw", base, base + 128 * step, step), False, False)
+    flag("pn", "eqs", 384, 512)
+    flag("pn3", "ru", 0, 384)
+    flag("pm", "mg", 0, 384, 1536, False, True)
+    ts(R("fl"), PF, 512.0, OP.is_gt)
+    k = len(links) // 4
+    tr = [RemoteDMATransfer(dst_ids=[dst(q)], dma_engine_mask=some(links[n * k:n * k + k]), remote_sem=T.sem.far,
+                            srcs=[ap(blk("fl", q, 128))], dsts=[ap(blk("flin", r, 128))]) for n, q in enumerate(others)]
+    remote("far", tr, 3 * k, 3 * k, [R("fl")], [blk("flin", q, 128) for q in others], 3.5)
+    for n, q in enumerate([r] + others):
+        src = blk("fl" if q == r else "flin", q, 128)
+        dma("a" if n % 2 else "s", "oflag", T.yflag[32 * q:32 * q + 32, :], ap(src), [src], [])
+    seps(3)
+    ts(R("sepo"), R("psW", 0, 32), 4096.0, OP.add)
+    tr = [RemoteDMATransfer(dst_ids=[dst(q) for q in others], dma_engine_mask=wide, remote_sem=T.sem.sar,
+                            srcs=[ap(R("sepo"))], dsts=[ap(blk("sepin", r, 32)) for _ in others])]
+    remote("sar", tr, len(links), 3 * len(links), [R("sepo")], [blk("sepin", q, 32) for q in others], 3.5)
+    for q in range(NR):
+        src = R("sepo") if q == r else blk("sepin", q, 32)
+        dma("s", "osep", T.ysep[2 * q:2 * q + 2, :], ap(src), [src], [])
 
     cnt, snap, recs = {}, {}, {}
     clock = {e: {} for e in eng}
@@ -576,22 +675,22 @@ def rank_program(g, core, T, topo):
 
     for x in schedule(tasks, bonus):
         e, kind, fn, sem, inc, reads, writes, _, _ = tasks[x]
-        reads = [q for q in reads if not q[0].startswith("token")]
-        writes = [q for q in writes if not q[0].startswith("token")]
         isdma = kind != "op"
         if kind != "land":
             best = {}
             for isw, rgs in ((False, reads), (True, writes)):
-                for buf, a, b in rgs:
-                    for c0, c1, w, e2, s2, v2, d2 in recs.get(buf, []):
-                        if c0 >= b or a >= c1:
+                for buf, a, b, pm in rgs:
+                    for c0, c1, p2, w, e2, s2, v2, d2 in recs.get(buf, []):
+                        if c0 >= b or a >= c1 or not pm & p2:
                             continue
                         if not isw and not w and not (buf.startswith("ps") and e2 != e):
                             continue
-                        if isw and e2 == e and not d2 and not isdma and (not w or e == "p"):
+                        if isw and e2 == e == "p":
                             continue
                         if s2 not in best or best[s2][0] < v2:
                             best[s2] = (v2, d2)
+            if e == "g" and kind == "op" and cnt.get("cg"):
+                best["cg"] = (cnt["cg"], False)
             for s2 in sorted(best, key=lambda z: (best[z][1], z)):
                 wait(e, s2, best[s2][0], best[s2][1])
         cnt[sem] = cnt.get(sem, 0) + inc
@@ -608,14 +707,18 @@ def rank_program(g, core, T, topo):
                 sn = snap.setdefault(sem, {})
                 for k, v in clock[e].items():
                     sn[k] = max(sn.get(k, 0), v)
-        for buf, a, b in writes:
+        for buf, a, b, pm in writes:
+            if buf.startswith("token"):
+                continue
             lst = recs.setdefault(buf, [])
-            lst[:] = [q for q in lst if not (a <= q[0] and q[1] <= b)]
-            lst.append((a, b, True, e, sem, cnt[sem], isdma))
-        for buf, a, b in reads:
+            lst[:] = [q for q in lst if not (a <= q[0] and q[1] <= b and not q[2] & ~pm)]
+            lst.append((a, b, pm, True, e, sem, cnt[sem], isdma))
+        for buf, a, b, pm in reads:
+            if buf.startswith("token"):
+                continue
             lst = recs.setdefault(buf, [])
-            lst[:] = [q for q in lst if not (not q[2] and q[4] == sem and a <= q[0] and q[1] <= b)]
-            lst.append((a, b, False, e, sem, cnt[sem], isdma))
+            lst[:] = [q for q in lst if not (not q[3] and q[5] == sem and a <= q[0] and q[1] <= b and not q[2] & ~pm)]
+            lst.append((a, b, pm, False, e, sem, cnt[sem], isdma))
 
     for sem, val in cnt.items():
         if clock["g"].get(sem, 0) < val:
@@ -630,21 +733,21 @@ def schedule(tasks, bonus):
     for x in range(n):
         e, kind, _, sem, _, reads, writes, _, _ = tasks[x]
         for isw, rgs in ((False, reads), (True, writes)):
-            for buf, a, b in rgs:
-                for c0, c1, w, e2, y in recs.get(buf, []):
-                    if c0 < b and a < c1 and (isw or w or (buf.startswith("ps") and e2 != e)):
+            for buf, a, b, pm in rgs:
+                for c0, c1, p2, w, e2, y in recs.get(buf, []):
+                    if c0 < b and a < c1 and pm & p2 and (isw or w or (buf.startswith("ps") and e2 != e)):
                         deps[x].add(y)
         for y in list(deps[x]):
             if tasks[y][1] == "dma":
                 deps[x].update(z for z in group[tasks[y][3]] if z < x)
         if kind == "dma":
             group.setdefault(sem, []).append(x)
-        for buf, a, b in writes:
+        for buf, a, b, pm in writes:
             lst = recs.setdefault(buf, [])
-            lst[:] = [q for q in lst if not (a <= q[0] and q[1] <= b)]
-            lst.append((a, b, True, e, x))
-        for buf, a, b in reads:
-            recs.setdefault(buf, []).append((a, b, False, e, x))
+            lst[:] = [q for q in lst if not (a <= q[0] and q[1] <= b and not q[2] & ~pm)]
+            lst.append((a, b, pm, True, e, x))
+        for buf, a, b, pm in reads:
+            recs.setdefault(buf, []).append((a, b, pm, False, e, x))
         deps[x].discard(x)
     succ = [[] for _ in range(n)]
     for x in range(n):
@@ -653,7 +756,7 @@ def schedule(tasks, bonus):
     prio = [0.0] * n
     for x in range(n - 1, -1, -1):
         prio[x] = tasks[x][8] + WAKE + max([prio[y] for y in succ[x]], default=0.0)
-    prio = [prio[x] + bonus.get(x, 0.0) for x in range(n)]
+    prio = [prio[x] + bonus[x] if bonus[x] >= 0 else bonus[x] for x in range(n)]
     left = [len(deps[x]) for x in range(n)]
     at = [0.0] * n
     free = {}
@@ -681,7 +784,7 @@ def schedule(tasks, bonus):
         end = st + tasks[x][8] + WAKE
         order.append(x)
         for y in succ[x]:
-            at[y] = max(at[y], end)
+            at[y] = max(at[y], end - WAKE if e == tasks[y][0] == "p" else end)
             left[y] -= 1
             if not left[y]:
                 ready.setdefault(tasks[y][0], []).append(y)

@@ -2,17 +2,18 @@ from concourse.bass import DstId, RemoteDMATransfer
 from concourse.mybir import AluOpType as OP, ActivationFunctionType as AF
 
 NR = 4
-ND = 8
-MATCH = "avavavavavaaaaaa"
-NE = 10
-WAY = "..G.G.G." "G..G..G." "G.G....." "GG.G..:."
-LAG = {".": 0, ":": 0, "g": 4.5, "G": 4.5, "x": 6.5, "X": 6.5}
-LIVE = "aav"
+ND = 9
+MATCH = "aavaavaavaavaava"
+NE = 16
+WAY = ".GHGGHGG" "GHGGHGG." "GGHGG..." "HGG..:.."
+LAG = {".": 0, ":": 0, "g": 4.5, "G": 4.5, "H": 4.5, "x": 6.5, "X": 6.5}
+HK = 2
+LIVE = "vvv"
 NEG = "v"
 MK0 = 2
 MK1 = 1
-NW = 7
-PREP = "aaa"
+NW = 9
+PREP = "aaav"
 NF = WAY.count("x") + WAY.count("X")
 BF, U2, F4, F2, I4 = "bfloat16", "uint16", "float32", "float16", "int32"
 SCRATCH = {}
@@ -42,7 +43,7 @@ for _t in range(NR):
     SEMAPHORES += ["%s%d" % (_k, _t) for _k in ("lx", "xa", "xp", "mdp", "ldp", "ndp", "mrg")]
 for _t in range(NF):
     SEMAPHORES += ["fa%d" % _t, "fb%d" % _t]
-SEMAPHORES += ["ga%d" % _t for _t in range(len(WAY)) if WAY[_t] in "gG"]
+SEMAPHORES += ["ga%d" % _t for _t in range(len(WAY)) if WAY[_t] in "gGH"]
 
 CY, GA, SC, PE = 0.86e-3, 1.56, 3.5, 0.43e-3
 WAKE, LAT, TRIP, ADD = 0.05, 2.2, 10.5, 5.5
@@ -56,9 +57,10 @@ for _t in range(NR):
     _k = 0
     while _k < len(_e):
         _n = 2 if (_t or _k) and _k + 1 < len(_e) and _e[_k + 1] == _e[_k] + 1 else 1
-        UNITS.append((_t, _e[_k], _n, sum(u[3] >= 0 for u in UNITS) if WAY[len(UNITS)] in "xX" else -1))
+        UNITS.append((_t, _e[_k], _n))
         _k += _n
 UNITS.append(UNITS.pop(-7))
+UNITS = [_u + (WAY[:_k].lower().count("x") if WAY[_k] in "xX" else -1,) for _k, _u in enumerate(UNITS)]
 
 
 def R(name, a=0, b=None, st=None, p=None):
@@ -225,6 +227,7 @@ def rank_program(g, core, T, topo):
             dma("sa"[t % 2], "ltv", ap(x), T.tv[own, 32 * t + 8 * c:32 * t + 8 * c + 8], [], [x], 4.0)
     lift[0] = 700.0
     stage(1, 4.4)
+    lift[0] = 650.0
     stage(2, 5.1)
     lift[0] = 2000.0
     for k, q in enumerate(others):
@@ -303,8 +306,10 @@ def rank_program(g, core, T, topo):
     places = ((1, 1), (129, 1), (258, 2), (516, 4))
     for c, (base, step) in enumerate(places):
         iota(R("ix", p=p32(c)), step, base, [token("xa2")], 0.4)
-    iota(MK, 0, 0, [token("xa2"), R("lm"), R("km"), R("bz"), R("qm"), R("v2"), R("ix")], 7.0)
-    dma("s", "ltb", ap(TB), ap(MK), [MK, XW], [TB], 5.0)
+    iota(TB, 0, 0, [token("xa2"), R("lm"), R("km"), R("bz"), R("qm"), R("v2"), R("ix")], 7.0)
+    lift[0] = 50.0
+    for k in range(8):
+        fill(blk("mk", k), 0.0)
 
     lift[0] = 450.0
     banks = [blk("psT", k) for k in range(4)] + [blk("psA", 0), blk("psA", 1), PF, PW]
@@ -349,15 +354,12 @@ def rank_program(g, core, T, topo):
         spread(bank, 64, "tz", 128 * t)
         ts(li(t, 0, 16), bank, 2048.0, OP.add)
 
-    for t in range(NR - 1):
-        lift[0] = (270.0, 230.0, 220.0)[t]
-        lists(t, (blk("psT", 0), PF, blk("psA", 0))[t])
-        if t == 0:
-            lift[0] = 250.0
-            for k in range(NR):
-                mm(blk("psW", k, 128), blk("bch", k, 128), blk("cy", k, 128))
-            tt(R("eq"), PW, R("cy"), OP.is_equal)
-            ts(R("inv"), R("cy"), 2048.0, OP.is_equal)
+    lists(0, blk("psT", 0))
+    lift[0] = 250.0
+    for k in range(NR):
+        mm(blk("psW", k, 128), blk("bch", k, 128), blk("cy", k, 128))
+    tt(R("eq"), PW, R("cy"), OP.is_equal)
+    ts(R("inv"), R("cy"), 2048.0, OP.is_equal)
 
     def match(j, bank):
         if MATCH[j] == "a":
@@ -372,8 +374,8 @@ def rank_program(g, core, T, topo):
             tt(blk("mt", j), bank, R("cy"), OP.is_equal)
 
     for j in range(NE):
-        lift[0] = 260.0
-        match(j, (blk("psA", 1), blk("psT", 1), blk("psT", 2))[j % 3])
+        lift[0] = 240.0
+        match(j, (blk("psA", 1), blk("psT", 1), blk("psT", 2), PF)[j % 4])
 
     def late_constants():
         lift[0] = 100.0
@@ -383,7 +385,6 @@ def rank_program(g, core, T, topo):
         copy("a", R("rowm", 0, 4), R("psT", 1536, 1540))
         for c in range(4):
             times(blk("sb", c, 128), R("psT", 1664, 1792), col("bc", c))
-        turn(4)
         last = col("rowm", 3)
         ts(col("rowm", 4), last, -512.0, OP.mult, 512.0, OP.add)
         ts(col("rowm", 5), last, 512.0, OP.mult, -512.0, OP.add)
@@ -432,7 +433,7 @@ def rank_program(g, core, T, topo):
         mm(ph, R("hi"), xv, True, False)
         mm(ph, R("nhi"), xy, False, True)
         act(hb, ph, AF.Abs)
-        if "g" in ways.lower():
+        if "g" in ways.lower() or "H" in ways:
             n1, n2 = blk("nh", 2 * b), blk("nh", 2 * b + 1)
             if NEG == "v":
                 ts(n1, hb, -1.0, OP.mult)
@@ -462,6 +463,10 @@ def rank_program(g, core, T, topo):
         if n == 1:
             for j in range(k):
                 gather_op(part(d, j), XW, li(t, i + j), slot("m", 0, 1), OP.subtract)
+        elif WAY[n] == "H":
+            turn(n - HK)
+            op("a", lambda q: q.activation(ap(d), ap(XW).indirect(ap(li(t, i, k))), AF.Copy), [XW, li(t, i, k)], [d, token("u%d" % n)],
+               gcost(li(t, i, k)))
         else:
             gather_op(d, XW, li(t, i, k), slot("m" if f < 0 else "lo", t % 2, k), OP.subtract, [token("u%d" % n)])
         if f >= 0:
@@ -478,15 +483,23 @@ def rank_program(g, core, T, topo):
         w = size[n] = slot("w", used["w"] % NW, k)
         used["w"] += 1
         turn(n)
-        act(w, slot("d", n % ND, k), AF.Abs)
-        if WAY[n] in "gG":
+        d = slot("d", n % ND, k)
+        if WAY[n] == "H":
+            z, d = d, slot("psT", used["psT"] % 2, k)
+            used["psT"] += 1
+            for j in range(k):
+                mm(part(d, j), R("nhi"), blk("xv", t % 2), True, False)
+                mm(part(d, j), R("nhi"), blk("xy", t % 2), False, False)
+                mm(part(d, j), R("im"), part(z, j), False, True)
+        act(w, d, AF.Abs)
+        if WAY[n] in "gGH":
             nh = slot("nh", t % 2, k)
             add("g", "dma", lambda q: q.dma_start(ap(w), ap(nh), accum_op=OP.add), "ga%d" % n, 16, [w, nh], [w], 1.0, ADD)
 
     def consume(n, c, lst):
         t, i, k, f = UNITS[n]
         d, s = slot("d", n % ND, k), slot("s", c % 3, k)
-        if WAY[n] in "gG":
+        if WAY[n] in "gGH":
             u = size[n]
         else:
             u = slot("psT", used["psT"] % 2, k)
@@ -500,7 +513,7 @@ def rank_program(g, core, T, topo):
                     mm(part(u, j), R("im"), part(d, j), True, False)
                     mm(part(u, j), R("n2"), part(slot("rb", f, k), j), False, True)
         turn(c + 1.5)
-        vec = WAY[n] in ":XG"
+        vec = WAY[n] in ":XGH"
         if vec:
             ts(s, u, -0.5, OP.max, 0.5, OP.min)
         else:
@@ -526,6 +539,7 @@ def rank_program(g, core, T, topo):
             HS = blk("hs", t, 128)
             mm(acc(t, 1), R("bm"), K)
             mm(acc(t, 2), R("qm"), K)
+            mm(acc(t, 3), R("im"), CY_)
             ts(HS, acc(t, 1), 0.0, OP.is_gt, col("rowm", t), OP.mult)
             ts(FI, acc(t, 2), -1.0, OP.is_equal)
             mark(t, HS)
@@ -533,15 +547,16 @@ def rank_program(g, core, T, topo):
             for c in (2, 3, 0, 1):
                 mm(blk("psA" if c else "psT", c, 128), blk("sb", c, 128), K)
             mm(acc(t, 2), R("qm"), K)
+            mm(acc(t, 3), R("im"), CY_)
             for c, (base, step) in enumerate(places):
                 if c:
                     act(R("hw", base, base + 128 * step, step), blk("psA", c, 128), AF.Sign)
                 else:
                     ts(R("hw", base, base + 128), blk("psT", 0, 128), 0.0, OP.is_gt)
             ts(FI, acc(t, 2), -1.0, OP.is_equal)
-        tt(FZ, FI, CY_, OP.mult)
-        mm(acc(t, 3), R("bm"), FZ)
-        tt(blk("eqs", t, 128), acc(t, 3), CY_, OP.is_equal)
+        tt(FZ, acc(t, 3), FI, OP.mult)
+        mm(acc(t, 1), R("bm"), FZ)
+        tt(blk("eqs", t, 128), acc(t, 1), CY_, OP.is_equal)
 
     def seps(t):
         for x in range(4):
@@ -561,24 +576,20 @@ def rank_program(g, core, T, topo):
     def flag(lhs, src, a, b, c0=0, start=False, stop=False):
         mm(R("psF", a, b), R(lhs), R(src, c0 + a, c0 + b), start, stop)
 
-    def after_two(c):
-        gather("a", R("rv"), TB, R("tvd"))
-        gather("a", blk("rk", 0, 128), TB, blk("yd", 0, 8))
+    def places_of_last():
+        gather("a", R("rv", 0, 384), TB, R("tvd", 0, 24))
+        gather("a", R("ru"), TB, R("yd", 0, 24))
         for k in range(6):
             for a in range(2):
-                mm(R("psW", 24 * a + k, 24 * a + 24, 6), blk("rv" if k > 2 else "rk", k % 3, 128), blk("w1", a, 4))
-        copy("v", R("tx"), R("psW", 0, 48))
-        spread(PW, 24, "tx", 0)
+                mm(R("psF", 24 * a + k, 24 * a + 24, 6), blk("rv" if k > 2 else "ru", k % 3, 128), blk("w1", a, 4))
+        copy("v", R("tx"), R("psF", 0, 48))
+        spread(PF, 24, "tx", 0)
         for b in range(4):
-            copy("v", R("xl", p=p32(b)), blk("psW", b, 48, p32(b)))
-        for s in range(2):
-            turn(c + 1 + s)
-            live(s, PW)
-            flag("pm", "mg", 0, 512, 512 * s)
+            copy("v", R("xl", p=p32(b)), blk("psF", b, 48, p32(b)))
 
     def after_three():
         gather("a", R("rv"), TB, R("tvd"))
-        gather("v", R("ry"), TB, R("yd", 0, 16))
+        gather(PREP[3], R("ry"), TB, R("yd", 0, 16))
         flag("gp", "hs", 0, 384)
         flag("pn", "eqs", 0, 384)
         flag("lpn", "rk", 256, 512)
@@ -586,9 +597,18 @@ def rank_program(g, core, T, topo):
         live(2, blk("psA", 0))
         flag("pm", "mg", 0, 512, 1024)
 
+    def after_two(c):
+        gather("a", R("rv"), TB, R("tvd"))
+        for s in range(2):
+            turn(c + s)
+            live(s, PW)
+            flag("pm", "mg", 0, 512, 512 * s)
+
     late_constants()
     lift[0] = 500.0
     prep(0)
+    turn(0)
+    lists(1, PF)
     order = sorted(range(len(UNITS)), key=lambda n: n + LAG[WAY[n]])
     made, seen = 0, []
     for c, n in enumerate(order):
@@ -609,9 +629,14 @@ def rank_program(g, core, T, topo):
             turn(c)
             passed(t)
         if c == 1:
+            turn(1)
+            places_of_last()
             for j in range(NE, 16):
                 turn(MK0 + MK1 * (j - NE))
                 match(j, PF)
+        if c == 5:
+            turn(6)
+            lists(2, PF)
         if c == 12:
             turn(c)
             lists(3, PF)
@@ -623,16 +648,20 @@ def rank_program(g, core, T, topo):
             turn(c - 4)
             look(t)
             if t == 2:
-                after_two(c - 2)
+                after_two(c)
             if t == 3:
                 for s in range(3):
                     seps(s)
+                turn(c + 2.3)
                 after_three()
         consume(n, c, n == mine[-1])
         seen.append(n)
         if n == mine[-1]:
             turn(c - 1)
             decide(t)
+    turn(len(UNITS) + 1)
+    seps(3)
+    ts(R("sepo"), R("psW", 0, 32), 4096.0, OP.add)
     turn(len(UNITS) + 2)
     HW = R("hw")
     gather("a", R("ru"), HW, R("xl", 0, 24))
@@ -650,8 +679,6 @@ def rank_program(g, core, T, topo):
     for n, q in enumerate([r] + others):
         src = blk("fl" if q == r else "flin", q, 128)
         dma("a" if n % 2 else "s", "oflag", T.yflag[32 * q:32 * q + 32, :], ap(src), [src], [])
-    seps(3)
-    ts(R("sepo"), R("psW", 0, 32), 4096.0, OP.add)
     tr = [RemoteDMATransfer(dst_ids=[dst(q) for q in others], dma_engine_mask=wide, remote_sem=T.sem.sar,
                             srcs=[ap(R("sepo"))], dsts=[ap(blk("sepin", r, 32)) for _ in others])]
     remote("sar", tr, len(links), 3 * len(links), [R("sepo")], [blk("sepin", q, 32) for q in others], 3.5)

from concourse.bass import DstId, RemoteDMATransfer
from concourse.mybir import AluOpType as OP, ActivationFunctionType as AF

NR = 4
ND = 9
MATCH = "aavaavaavaavaava"
NE = 16
WAY = ".GHGGHGG" "GHGGHGG." "GGHGG..." "HGG..:.."
LAG = {".": 0, ":": 0, "g": 4.5, "G": 4.5, "H": 4.5, "x": 6.5, "X": 6.5}
HK = 2
LIVE = "vvv"
NEG = "v"
MK0 = 2
MK1 = 1
NW = 9
PREP = "aaav"
NF = WAY.count("x") + WAY.count("X")
BF, U2, F4, F2, I4 = "bfloat16", "uint16", "float32", "float16", "int32"
SCRATCH = {}
for _n, _w, _d in (
        ("xst", 3072, BF), ("xin", 3072, BF), ("xs", 4112, BF), ("tvs", 32, I4), ("tvd", 32, U2),
        ("adjq", 1024, I4), ("adjh", 1024, F2), ("adjw", 4096, F4), ("ones", 128, BF),
        ("a0", 128, BF), ("a1", 128, BF), ("pm", 128, BF), ("im", 128, BF), ("b1", 128, BF), ("bm", 128, BF), ("lt", 128, BF),
        ("k1", 128, BF), ("km", 128, BF), ("z1", 128, BF), ("bz", 192, BF), ("g1", 128, BF), ("gm", 128, BF),
        ("l1", 128, BF), ("lm", 128, BF), ("r32", 128, BF), ("r16", 16, F4), ("rowm", 8, F4), ("bc", 8, F4),
        ("gs", 240, BF), ("gs2", 240, BF), ("nbz", 192, BF), ("sel", 2048, BF), ("bch", 2048, BF), ("bs", 384, BF),
        ("pi", 128, BF), ("hi", 128, BF), ("nhi", 128, BF), ("ni", 128, BF), ("n2", 128, BF),
        ("q16", 128, BF), ("qm", 128, BF), ("lk", 128, BF), ("pn", 128, BF), ("lpn", 128, BF), ("gp", 128, BF),
        ("ix", 128, BF), ("ixs", 128, BF), ("v2", 128, BF), ("w1", 8, BF), ("gq", 512, BF), ("sb", 512, BF), ("pn3", 128, BF),
        ("cv", 512, F2), ("cy", 512, F2), ("ty", 64, F2), ("tz", 512, F2), ("yx", 128, U2), ("yd", 32, U2), ("li", 2048, U2),
        ("eq", 512, BF), ("inv", 512, BF), ("mt", 8192, BF), ("mk", 4096, BF), ("tb", 4096, BF),
        ("rk", 512, BF), ("ry", 256, BF), ("rv", 512, BF), ("mg", 2048, BF), ("ok", 128, BF), ("hs", 384, BF),
        ("tx", 48, F2), ("xl", 48, U2), ("hw", 1040, BF), ("ru", 384, BF),
        ("fi", 512, F2), ("fz", 512, F2), ("eqs", 512, BF), ("fl", 512, BF), ("flin", 512, BF), ("sepo", 32, F4),
        ("sepin", 128, F4), ("xv", 1024, BF), ("xy", 1024, BF), ("m", 2048, F4), ("lo", 2048, BF), ("hh", 2048, BF),
        ("d", 1024 * ND, BF), ("s", 3072, BF), ("w", 1024 * NW, BF), ("nh", 2048, BF), ("rb", 1024 * max(NF, 1), BF)):
    SCRATCH[_n] = ("sbuf", [128, _w], _d)
for _n, _w in (("psT", 2048), ("psA", 1024), ("psF", 512), ("psW", 512)):
    SCRATCH[_n] = ("psum", [128, _w], F4)

SEMAPHORES = ["cv", "ca", "cp", "cg", "ltv", "ladj", "lown", "ltb", "loc", "sar", "far", "osep", "oflag"]
for _t in range(NR):
    SEMAPHORES += ["%s%d" % (_k, _t) for _k in ("lx", "xa", "xp", "mdp", "ldp", "ndp", "mrg")]
for _t in range(NF):
    SEMAPHORES += ["fa%d" % _t, "fb%d" % _t]
SEMAPHORES += ["ga%d" % _t for _t in range(len(WAY)) if WAY[_t] in "gGH"]

CY, GA, SC, PE = 0.86e-3, 1.56, 3.5, 0.43e-3
WAKE, LAT, TRIP, ADD = 0.05, 2.2, 10.5, 5.5
XL = (6.0, 6.0, 7.5)
ALL = (1 << 128) - 1
BIG = 1.5 * 2 ** 27

UNITS = []
for _t in range(NR):
    _e = [_i for _i in range(16) if _i != _t]
    _k = 0
    while _k < len(_e):
        _n = 2 if (_t or _k) and _k + 1 < len(_e) and _e[_k + 1] == _e[_k] + 1 else 1
        UNITS.append((_t, _e[_k], _n))
        _k += _n
UNITS.append(UNITS.pop(-7))
UNITS = [_u + (WAY[:_k].lower().count("x") if WAY[_k] in "xX" else -1,) for _k, _u in enumerate(UNITS)]


def R(name, a=0, b=None, st=None, p=None):
    return (name, a, SCRATCH[name][1][1] if b is None else b, st, p)


def region(x):
    if x[0].startswith("ps"):
        return (x[0], x[1] // 512 * 512, (x[2] + 511) // 512 * 512, ALL)
    if len(x) < 5 or x[4] is None:
        return (x[0], x[1], x[2], ALL)
    return (x[0], x[1], x[2], sum(1 << k for k in range(x[4][0], x[4][1], x[4][2] or 1)))


def place(topo, c):
    a = topo.addr(c)
    return DstId(rid=a[0], pnc=a[1])


def helper(topo, T, c):
    return [k for k in topo.cores_of(c) if T.rank_of(k) is None and topo.die(k) == topo.die(c)][0]


def hand_back(g, core, T, topo, home):
    n = len(topo.engines(core, home))
    for t, i, k, f in UNITS:
        if f >= 0:
            x = T.rb[:, 1024 * f:1024 * f + 512 * k]
            g.wait_ge(T.sem["fa%d" % f], n)
            g.remote_dma_fused([RemoteDMATransfer(dst_ids=[place(topo, home)], dma_engine_mask=topo.mask(core, home),
                                                  remote_sem=T.sem["fb%d" % f], srcs=[x], dsts=[x])], local_sem=T.sem.loc)
    g.wait_ge(T.sem.loc, n * NF)


def rank_program(g, core, T, topo):
    r = T.rank_of(core)
    if r is None:
        for c in T.cores:
            if NF and helper(topo, T, c) == core:
                hand_back(g, core, T, topo, c)
        return
    eng = {"v": g.vector, "a": g.scalar, "p": g.tensor, "g": g, "s": g.sync}
    tasks = []
    bonus, lift = {}, [0.0]

    def add(e, kind, fn, sem, inc, reads, writes, busy, lat):
        bonus[len(tasks)] = lift[0]
        tasks.append((e, kind, fn, sem, inc, [region(x) for x in reads], [region(x) for x in writes], busy, lat))

    def turn(k):
        lift[0] = -100.0 - k

    def op(e, fn, reads, writes, cost):
        add(e, "op", fn, "c" + e, 1, reads, writes, cost, cost)

    def dma(e, sem, out, in_, reads, writes, lat=LAT):
        add(e, "dma", lambda q: q.dma_start(out, in_), sem, 16, reads, writes, 0.1, lat)

    def ap(x):
        p = x[4] or (0, 128, None)
        return T[x[0]][p[0]:p[1]:p[2], x[1]:x[2]:x[3]]

    def blk(name, k, w=512, p=None):
        return R(name, w * k, w * k + w, None, p)

    def col(name, k):
        return R(name, k, k + 1)

    def p32(b):
        return (32 * b, 32 * b + 32, None)

    def num(x):
        return len(range(x[1], x[2], x[3] or 1))

    def small(*xs):
        return all(SCRATCH[x[0]][0] == "sbuf" and SCRATCH[x[0]][2] in (BF, U2, F2) for x in xs)

    def vc(n, f=1.0):
        return 0.02 + max(64, n * f) * CY

    def copy(e, out, in_):
        if e == "v":
            op("v", lambda q: q.tensor_copy(ap(out), ap(in_)), [in_], [out], vc(num(in_), 0.5 if small(out, in_) else 1))
        else:
            act(out, in_, AF.Copy)

    def act(out, in_, func):
        op("a", lambda q: q.activation(ap(out), ap(in_), func), [in_], [out], 0.05 + num(in_) * CY)

    def times(out, in_, s, func=AF.Copy):
        cols, f = ([s], ap(s)) if isinstance(s, tuple) else ([], s)
        op("a", lambda q: q.activation(ap(out), ap(in_), func, scale=f), [in_] + cols, [out], 0.05 + num(in_) * CY)

    def tt(out, a, b, o):
        f = 1 if a[0].startswith("ps") or b[0].startswith("ps") else 2
        op("v", lambda q: q.tensor_tensor(ap(out), ap(a), ap(b), o), [a, b], [out], vc(num(a), f))

    def ts(out, a, s1, o1, s2=None, o2=None):
        cols = [x for x in (s1, s2) if isinstance(x, tuple)]
        s1, s2 = [ap(x) if isinstance(x, tuple) else x for x in (s1, s2)]
        args = (s1, s2, o1) if o2 is None else (s1, s2, o1, o2)
        op("v", lambda q: q.tensor_scalar(ap(out), ap(a), *args), [a] + cols, [out], vc(num(a), 0.5 if small(out, a) else 1))

    def gcost(off):
        return 0.07 + 16 * num(off) * GA * CY

    def gather(e, out, win, off, after=()):
        if e == "v":
            op("v", lambda q: q.tensor_copy(ap(out), ap(win).indirect(ap(off))), [win, off, *after], [out], gcost(off))
        else:
            op("a", lambda q: q.activation(ap(out), ap(win).indirect(ap(off)), AF.Copy), [win, off, *after], [out], gcost(off))

    def gather_op(out, win, off, other, o, done=()):
        op("v", lambda q: q.tensor_tensor(ap(out), ap(win).indirect(ap(off)), ap(other), o), [win, off, other], [out, *done], gcost(off))

    def scatter(win, off, src):
        op("v", lambda q: q.tensor_copy(ap(win).indirect(ap(off)), ap(src)), [off, src], [win], 0.07 + num(src) * SC * CY)

    def mm(out, lhs, rhs, start=True, stop=True):
        op("p", lambda q: q.matmul(ap(out), ap(lhs), ap(rhs), start, stop), [lhs, rhs], [out], 0.015 + max(64, num(rhs)) * PE)

    def fill(x, val):
        op("v", lambda q: q.memset(ap(x), val), [], [x], vc(num(x), 0.5))

    def asel(out, in_, pat, cmp, base, cm, other=0.0):
        op("g", lambda q: q.affine_select(ap(out), ap(in_), pat, cmp, other, base, cm), [in_], [out], 0.2 + 2 * CY * num(in_))

    def token(name):
        return ("token" + name, 0, 1)

    def dst(q):
        return place(topo, T.cores[q])

    def some(engines):
        return sum(1 << e for e in engines)

    def remote(name, transfers, nloc, nrem, srcs, land, lat):
        add("g", "send", lambda q: q.remote_dma_fused(transfers, local_sem=T.sem.loc), "loc", nloc, srcs, [token(name)], 0.6, 0.6)
        add(None, "land", None, name, nrem, [token(name)] + srcs, land, 0.0, lat)

    XW, AW, MK, TB = R("xs"), R("adjw"), R("mk"), R("tb")
    PW, PF = R("psW"), R("psF")
    others = [(r + 1 + k) % NR for k in range(NR - 1)]
    links = topo.engines(core, T.cores[others[0]])
    wide = topo.mask(core, T.cores[others[0]])
    mate = helper(topo, T, core)
    near = topo.engines(core, mate)
    own = slice(32 * r, 32 * r + 32)

    def stage(k, lat):
        q = others[k]
        dma("s", "lx%d" % k, ap(blk("xst", k, 1024)), T.x[32 * q:32 * q + 32, :], [], [blk("xst", k, 1024)], lat)

    lift[0] = 1000.0
    stage(0, 3.0)
    lift[0] = 800.0
    for b in range(4):
        x = R("adjq", p=p32(b))
        dma("a", "ladj", ap(x), T.adj[own, 1024 * b:1024 * b + 1024], [], [x], 4.2)
    lift[0] = 750.0
    for t in range(NR):
        for c in range(4):
            x = blk("tvs", t, 8, p32(c))
            dma("sa"[t % 2], "ltv", ap(x), T.tv[own, 32 * t + 8 * c:32 * t + 8 * c + 8], [], [x], 4.0)
    lift[0] = 700.0
    stage(1, 4.4)
    lift[0] = 650.0
    stage(2, 5.1)
    lift[0] = 2000.0
    for k, q in enumerate(others):
        tr = [RemoteDMATransfer(dst_ids=[dst(q)], dma_engine_mask=wide, remote_sem=T.sem["xa%d" % k],
                                srcs=[ap(blk("xst", k, 1024))], dsts=[ap(blk("xin", k, 1024))])]
        remote("xa%d" % k, tr, len(links), len(links), [blk("xst", k, 1024)], [blk("xin", k, 1024)], XL[k])
    x = R("xs", 0, 4096, p=p32(r))
    dma("s", "lown", ap(x), T.x[own, :], [blk("xin", 0, 1024)], [x], 3.5)
    for k in range(NR - 1):
        x = R("xs", 0, 4096, p=p32((r - 1 - k) % NR))
        dma("s", "xp%d" % k, ap(x), ap(blk("xin", k, 1024)), [blk("xin", k, 1024)], [x], 3.0)

    one = R("ones")
    lift[0] = 600.0
    fill(one, 1.0)
    asel(R("a0"), one, [[0, 4], [-1, 32]], OP.is_equal, 0, 1)
    asel(R("a1"), one, [[0, 4], [-1, 32]], OP.is_equal, 16, 1)
    lift[0] = 500.0
    asel(R("pm"), one, [[-16, 2], [-1, 16], [-32, 4]], OP.is_equal, 0, 1)
    asel(R("im"), one, [[-1, 128]], OP.is_equal, 0, 1)
    asel(R("b1"), one, [[-16, 8], [0, 16]], OP.is_ge, 0, 1)
    asel(R("bm"), R("b1"), [[16, 8], [0, 16]], OP.is_ge, 15, -1)
    p16 = (0, 16, None)
    half = [R("a0", p=p16), R("a1", p=p16)]
    lift[0] = 600.0
    mm(blk("psF", 0, 128), R("a0", p=p32(0)), R("a0", p=p32(0)))
    copy("v", R("r32"), blk("psF", 0, 128))
    for u in range(2):
        for a in range(2):
            mm(blk("psW", 2 * u + a, 128), half[u], half[a])
    lift[0] = 400.0
    fill(R("bc"), 0.0)
    for b in range(4):
        fill(R("bc", b, b + 1, p=p32(b)), 1.0)
        fill(R("bc", 4 + b, 5 + b, p=p32(b)), 32.0)
    for b in range(4):
        ts(blk("sel", b), PW, col("bc", b), OP.mult)
    for a in range(2):
        mm(R("psA", 0, 16), half[a], R("im", 0, 16, p=p16), a == 0, a == 1)
    for a in range(2):
        mm(R("psA", 16 + a, 17 + a), half[a], R("ones", 0, 1, p=p16))
    fill(R("gs"), 0.0)
    copy("a", R("r16"), R("psA", 0, 16))
    copy("a", R("gs", 111, 128, 16), R("psA", 16, 18))
    for nm, f in (("ni", -1.0), ("hi", 0.5), ("nhi", -0.5), ("pi", 512.0), ("n2", -2.0)):
        times(R(nm), R("im"), f)
    lift[0] = 300.0
    for j in range(16):
        if j % 2:
            times(blk("bch", j, 128), R("bm"), col("r16", j))
        else:
            ts(blk("bch", j, 128), R("bm"), col("r16", j), OP.mult)
    fill(R("xs", 4096, 4112), 0.0)
    fill(R("bz"), 0.0)
    fill(R("hw"), 0.0)
    lift[0] = 500.0
    copy("v", R("tvd"), R("tvs"))

    lift[0] = 0.0
    asel(R("lt"), R("bm"), [[1, 128]], OP.is_gt, 0, -1)
    asel(R("k1"), R("bm"), [[-16, 8], [-4, 16]], OP.is_ge, 0, 1)
    asel(R("km"), R("k1"), [[16, 8], [4, 16]], OP.is_ge, 3, -1)
    asel(R("z1"), one, [[-16, 2], [-32, 16], [-1000, 4]], OP.is_ge, 0, 1)
    asel(R("bz", 51, 179), R("z1"), [[16, 2], [32, 16], [1000, 4]], OP.is_ge, 15, -1)
    asel(R("g1"), one, [[-16, 2], [0, 16], [-32, 4]], OP.is_ge, 0, 1)
    asel(R("gm"), R("g1"), [[16, 2], [0, 16], [32, 4]], OP.is_ge, 15, -1)
    asel(R("l1"), R("gm"), [[-16, 2], [-4, 16], [-32, 4]], OP.is_ge, 0, 1)
    asel(R("lm"), R("l1"), [[16, 2], [4, 16], [32, 4]], OP.is_ge, 3, -1)
    asel(R("v2"), one, [[0, 4], [-1, 2], [0, 16]], OP.is_equal, 0, 1)
    times(R("q16"), R("lt"), 16.0)
    asel(R("qm"), R("q16"), [[-1, 128]], OP.not_equal, 0, 1, -1.0)

    def iota(x, step, base, after, cost):
        op("g", lambda q: q.iota(ap(x), [[step, num(x)]], base, 0, allow_small_or_imprecise_dtypes=True), after, [x], cost)

    places = ((1, 1), (129, 1), (258, 2), (516, 4))
    for c, (base, step) in enumerate(places):
        iota(R("ix", p=p32(c)), step, base, [token("xa2")], 0.4)
    iota(TB, 0, 0, [token("xa2"), R("lm"), R("km"), R("bz"), R("qm"), R("v2"), R("ix")], 7.0)
    lift[0] = 50.0
    for k in range(8):
        fill(blk("mk", k), 0.0)

    lift[0] = 450.0
    banks = [blk("psT", k) for k in range(4)] + [blk("psA", 0), blk("psA", 1), PF, PW]
    for h in range(2):
        ts(blk("adjh", h), blk("adjq", h), -2048.0, OP.add)
        for b in range(4):
            mm(banks[4 * h + b], R("r32", p=p32(b)), blk("adjh", h, 512, p32(b)))
    for h in range(2):
        for b in range(4):
            copy("v" if 4 * h + b in (3, 5, 7) else "a", blk("adjw", 2 * b + h), banks[4 * h + b])

    def spread(bank, n, rows, c0):
        for w in range(8):
            for a in range(2):
                mm(R(bank[0], bank[1] + w, bank[1] + 8 * n, 8), blk("sel", 2 * w + a, 128),
                   R(rows, c0 + n * a, c0 + n * a + n), a == 0, a == 1)

    def li(t, i, n=1):
        return R("li", 512 * t + 32 * i, 512 * t + 32 * i + 32 * n)

    gather("v", R("cv"), AW, R("tvd"))
    for t in range(NR):
        for a in range(2):
            mm(R("psW", 16 * a + t, 16 * a + 16, 4), blk("cv", t, 128), R("pm", 64 * a + 4 * t, 64 * a + 4 * t + 4))
    copy("v", R("ty", 0, 32), R("psW", 0, 32))
    spread(PF, 16, "ty", 0)
    for c in range(4):
        ts(R("yd", p=p32(c)), blk("psF", c, 32, p32(c)), 2048.0, OP.add)
    gather("v", R("cy"), AW, R("yd"))
    lift[0] = 250.0
    for t in range(NR):
        for a in range(2):
            mm(R("psT", 16 * a + 4 * t, 16 * a + 4 * t + 4), blk("cv", t, 128), R("pm", 64 * a + 4 * t, 64 * a + 4 * t + 4))
    copy("v", R("ty", 32, 64), R("psT", 0, 32))
    spread(blk("psA", 0), 16, "ty", 32)
    ts(R("yx"), R("psA", 0, 128), 2048.0, OP.add)
    lift[0] = 270.0
    for t in range(NR):
        mm(blk("psW", t, 128), blk("cy", t, 128), R("pm"))
    copy("v", R("tz"), PW)
    def lists(t, bank):
        spread(bank, 64, "tz", 128 * t)
        ts(li(t, 0, 16), bank, 2048.0, OP.add)

    lists(0, blk("psT", 0))
    lift[0] = 250.0
    for k in range(NR):
        mm(blk("psW", k, 128), blk("bch", k, 128), blk("cy", k, 128))
    tt(R("eq"), PW, R("cy"), OP.is_equal)
    ts(R("inv"), R("cy"), 2048.0, OP.is_equal)

    def match(j, bank):
        if MATCH[j] == "a":
            mm(bank, blk("bch", j, 128), R("cv"), True, False)
            mm(bank, R("ni"), R("cy"), False, True)
            copy("a", blk("mt", j), bank)
            if j < NE:
                turn(2 + j)
            ts(blk("mt", j), blk("mt", j), 0.0, OP.is_equal)
        else:
            mm(bank, blk("bch", j, 128), R("cv"))
            tt(blk("mt", j), bank, R("cy"), OP.is_equal)

    for j in range(NE):
        lift[0] = 240.0
        match(j, (blk("psA", 1), blk("psT", 1), blk("psT", 2), PF)[j % 4])

    def late_constants():
        lift[0] = 100.0
        mm(R("psT", 1536, 1540), half[0], R("km", 0, 4, p=p16), True, False)
        mm(R("psT", 1536, 1540), half[1], R("km", 0, 4, p=p16), False, True)
        mm(R("psT", 1664, 1792), R("v2", p=p16), R("v2", p=p16))
        copy("a", R("rowm", 0, 4), R("psT", 1536, 1540))
        for c in range(4):
            times(blk("sb", c, 128), R("psT", 1664, 1792), col("bc", c))
        last = col("rowm", 3)
        ts(col("rowm", 4), last, -512.0, OP.mult, 512.0, OP.add)
        ts(col("rowm", 5), last, 512.0, OP.mult, -512.0, OP.add)
        ts(col("rowm", 6), col("r16", 3), -512.0, OP.mult)
        for nm, src, f in (("pn", "pm", -512.0), ("gp", "gm", 128.0), ("nbz", "bz", -2048.0), ("gs2", "gs", 2.0), ("lk", "km", col("rowm", 4)),
                           ("lpn", "lm", col("rowm", 5)), ("pn3", "pm", col("rowm", 6)), ("ixs", "ix", last)):
            times(R(nm), R(src), f)
        for c in range(4):
            times(blk("gq", c, 128), R("gm"), col("bc", 4 + c))
        for s in range(NR - 1):
            times(blk("bs", s, 128), R("bm"), col("rowm", s))
        for a in range(2):
            times(blk("w1", a, 4), R("gm", 64 * a, 64 * a + 4), last)
        mark(3, R("ixs"))

    def mark(t, src):
        scatter(MK, blk("tvd", t, 8), src)
        scatter(MK, blk("yd", t, 8), src)
        for a in range(2):
            for c in range(4):
                z = 16 * a + 4 * t
                out, rows = R("tb", p=(z + c, 128, 32)), R("mk", p=(32 * c + z, 32 * c + z + 4, None))
                dma("s", "mrg%d" % t, ap(out), ap(rows), [rows], [out], LAT + 0.6)

    def prep(t, after=()):
        b = t % 2
        xv, xy, hb = blk("xv", b), blk("xy", b), blk("hh", t)
        m1, m2, l1, l2 = blk("m", 2 * b), blk("m", 2 * b + 1), blk("lo", 2 * b), blk("lo", 2 * b + 1)
        ph = PW if t else blk("psT", 3)
        ways = WAY[8 * t:8 * t + 8]
        if t:
            gather(PREP[0], xv, XW, li(t, t), after)
            gather(PREP[1], xy, XW, blk("yx", t, 32), after)
            mm(PW, R("hi"), xv, True, False)
            mm(PW, R("hi"), xy, False, True)
            copy(PREP[2], m1, PW)
            dma("s", "mdp%d" % t, ap(m2), ap(m1), [m1], [m2], LAT + 0.6)
        else:
            for h, bank in enumerate((R("psW", 0, 256), R("psA", 512, 768))):
                gather("a", blk("xv", h, 256), XW, blk("li", h, 16))
                gather("v", blk("xy", h, 256), XW, blk("yx", h, 16))
                mm(bank, R("hi"), blk("xv", h, 256), True, False)
                mm(bank, R("hi"), blk("xy", h, 256), False, True)
                copy("av"[h], blk("m", h, 256), bank)
            dma("s", "mdp0", ap(m2), ap(m1), [m1], [m2], LAT + 0.6)
        mm(ph, R("hi"), xv, True, False)
        mm(ph, R("nhi"), xy, False, True)
        act(hb, ph, AF.Abs)
        if "g" in ways.lower() or "H" in ways:
            n1, n2 = blk("nh", 2 * b), blk("nh", 2 * b + 1)
            if NEG == "v":
                ts(n1, hb, -1.0, OP.mult)
            else:
                times(n1, hb, -1.0)
            dma("s", "ndp%d" % t, ap(n2), ap(n1), [n1], [n2], LAT + 0.3)
        if "x" in ways.lower():
            mm(PW, R("hi"), xv, True, False)
            mm(PW, R("hi"), xy, False, False)
            mm(PW, R("ni"), hb, False, True)
            copy("a", l1, PW)
            dma("s", "ldp%d" % t, ap(l2), ap(l1), [l1], [l2], LAT + 0.3)

    def acc(t, k=0):
        return R("psA", 512 * (t % 2) + 128 * k, 512 * (t % 2) + 128 * k + 128)

    def slot(name, n, k):
        return R(name, 1024 * n, 1024 * n + 512 * k)

    def part(x, j):
        return R(x[0], x[1] + 512 * j, x[1] + 512 * j + 512)

    def produce(n):
        t, i, k, f = UNITS[n]
        d = slot("d", n % ND, k)
        turn(n - 2)
        if n == 1:
            for j in range(k):
                gather_op(part(d, j), XW, li(t, i + j), slot("m", 0, 1), OP.subtract)
        elif WAY[n] == "H":
            turn(n - HK)
            op("a", lambda q: q.activation(ap(d), ap(XW).indirect(ap(li(t, i, k))), AF.Copy), [XW, li(t, i, k)], [d, token("u%d" % n)],
               gcost(li(t, i, k)))
        else:
            gather_op(d, XW, li(t, i, k), slot("m" if f < 0 else "lo", t % 2, k), OP.subtract, [token("u%d" % n)])
        if f >= 0:
            e = len(near) // k
            tr = [RemoteDMATransfer(dst_ids=[place(topo, mate)], dma_engine_mask=some(near[j * e:j * e + e]), remote_sem=T.sem["fa%d" % f],
                                    srcs=[ap(part(d, j)), ap(blk("hh", t))], dsts=[ap(part(slot("rb", f, k), j))], alu_op=3)
                  for j in range(k)]
            remote("fb%d" % f, tr, len(near), len(near), [d, blk("hh", t)], [slot("rb", f, k)], TRIP)

    used, size = {"w": 0, "psT": 0}, {}

    def absolute(n):
        t, i, k, f = UNITS[n]
        w = size[n] = slot("w", used["w"] % NW, k)
        used["w"] += 1
        turn(n)
        d = slot("d", n % ND, k)
        if WAY[n] == "H":
            z, d = d, slot("psT", used["psT"] % 2, k)
            used["psT"] += 1
            for j in range(k):
                mm(part(d, j), R("nhi"), blk("xv", t % 2), True, False)
                mm(part(d, j), R("nhi"), blk("xy", t % 2), False, False)
                mm(part(d, j), R("im"), part(z, j), False, True)
        act(w, d, AF.Abs)
        if WAY[n] in "gGH":
            nh = slot("nh", t % 2, k)
            add("g", "dma", lambda q: q.dma_start(ap(w), ap(nh), accum_op=OP.add), "ga%d" % n, 16, [w, nh], [w], 1.0, ADD)

    def consume(n, c, lst):
        t, i, k, f = UNITS[n]
        d, s = slot("d", n % ND, k), slot("s", c % 3, k)
        if WAY[n] in "gGH":
            u = size[n]
        else:
            u = slot("psT", used["psT"] % 2, k)
            used["psT"] += 1
            turn(c + 1)
            for j in range(k):
                if f < 0:
                    mm(part(u, j), R("ni"), blk("hh", t), True, False)
                    mm(part(u, j), R("im"), part(size[n], j), False, True)
                else:
                    mm(part(u, j), R("im"), part(d, j), True, False)
                    mm(part(u, j), R("n2"), part(slot("rb", f, k), j), False, True)
        turn(c + 1.5)
        vec = WAY[n] in ":XGH"
        if vec:
            ts(s, u, -0.5, OP.max, 0.5, OP.min)
        else:
            act(s, u, AF.Sign)
        turn(c + 2.2)
        for j in range(k):
            for b in range(4):
                z, a = 111 - 32 * b - i - j, s[1] + 512 * j + 128 * b
                mm(acc(t), R("gs2" if vec else "gs", z, z + 128), R("s", a, a + 128), False, lst and j == k - 1 and b == 3)

    def passed(t):
        mm(acc(t), R("pi"), blk("eq", t, 128), True, False)
        mm(acc(t), R("pi"), blk("inv", t, 128), False, False)

    def look(t):
        gather("a", blk("rk", t, 128), TB, blk("yd", t, 8))
        mm(acc(t), R("lk"), blk("rk", t, 128), False, False)

    def decide(t):
        K, FI, FZ, CY_ = R("ok"), blk("fi", t, 128), blk("fz", t, 128), blk("cy", t, 128)
        ts(K, acc(t), BIG, OP.add, BIG, OP.is_equal)
        if t < 3:
            HS = blk("hs", t, 128)
            mm(acc(t, 1), R("bm"), K)
            mm(acc(t, 2), R("qm"), K)
            mm(acc(t, 3), R("im"), CY_)
            ts(HS, acc(t, 1), 0.0, OP.is_gt, col("rowm", t), OP.mult)
            ts(FI, acc(t, 2), -1.0, OP.is_equal)
            mark(t, HS)
        else:
            for c in (2, 3, 0, 1):
                mm(blk("psA" if c else "psT", c, 128), blk("sb", c, 128), K)
            mm(acc(t, 2), R("qm"), K)
            mm(acc(t, 3), R("im"), CY_)
            for c, (base, step) in enumerate(places):
                if c:
                    act(R("hw", base, base + 128 * step, step), blk("psA", c, 128), AF.Sign)
                else:
                    ts(R("hw", base, base + 128), blk("psT", 0, 128), 0.0, OP.is_gt)
            ts(FI, acc(t, 2), -1.0, OP.is_equal)
        tt(FZ, acc(t, 3), FI, OP.mult)
        mm(acc(t, 1), R("bm"), FZ)
        tt(blk("eqs", t, 128), acc(t, 1), CY_, OP.is_equal)

    def seps(t):
        for x in range(4):
            z, a = 51 - 16 * t - x, 128 * t + 32 * x
            mm(R("psW", 0, 32), R("bz", z, z + 128), R("fz", a, a + 32), t == 0 and x == 0, False)
            mm(R("psW", 0, 32), R("nbz", z, z + 128), R("fi", a, a + 32), False, t == 3 and x == 3)

    def live(s, bank):
        if LIVE[s] == "v":
            mm(bank, blk("bs", s, 128), R("rv"))
            tt(blk("mg", s), bank, blk("mt", s), OP.is_lt)
        else:
            mm(bank, blk("bs", s, 128), R("rv"), True, False)
            mm(bank, R("ni"), blk("mt", s), False, True)
            times(blk("mg", s), bank, -1.0, AF.Relu)

    def flag(lhs, src, a, b, c0=0, start=False, stop=False):
        mm(R("psF", a, b), R(lhs), R(src, c0 + a, c0 + b), start, stop)

    def places_of_last():
        gather("a", R("rv", 0, 384), TB, R("tvd", 0, 24))
        gather("a", R("ru"), TB, R("yd", 0, 24))
        for k in range(6):
            for a in range(2):
                mm(R("psF", 24 * a + k, 24 * a + 24, 6), blk("rv" if k > 2 else "ru", k % 3, 128), blk("w1", a, 4))
        copy("v", R("tx"), R("psF", 0, 48))
        spread(PF, 24, "tx", 0)
        for b in range(4):
            copy("v", R("xl", p=p32(b)), blk("psF", b, 48, p32(b)))

    def after_three():
        gather("a", R("rv"), TB, R("tvd"))
        gather(PREP[3], R("ry"), TB, R("yd", 0, 16))
        flag("gp", "hs", 0, 384)
        flag("pn", "eqs", 0, 384)
        flag("lpn", "rk", 256, 512)
        flag("lpn", "ry", 0, 256)
        live(2, blk("psA", 0))
        flag("pm", "mg", 0, 512, 1024)

    def after_two(c):
        gather("a", R("rv"), TB, R("tvd"))
        for s in range(2):
            turn(c + s)
            live(s, PW)
            flag("pm", "mg", 0, 512, 512 * s)

    late_constants()
    lift[0] = 500.0
    prep(0)
    turn(0)
    lists(1, PF)
    order = sorted(range(len(UNITS)), key=lambda n: n + LAG[WAY[n]])
    made, seen = 0, []
    for c, n in enumerate(order):
        while made < len(UNITS) and (made <= n or made <= c + 2) and (made < ND or made - ND in seen):
            t = UNITS[made][0]
            k = made - [u[0] for u in UNITS].index(t)
            if k == 3 and t < 3:
                turn(made)
                prep(t + 1, [token("u%d" % (made - 1))])
            produce(made)
            made += 1
        for z in range(made):
            if WAY[z] not in "xX" and z not in size and (z <= n + LAG[WAY[n]] + 1):
                absolute(z)
        t = UNITS[n][0]
        mine = [z for z in order if UNITS[z][0] == t]
        if n == mine[0]:
            turn(c)
            passed(t)
        if c == 1:
            turn(1)
            places_of_last()
            for j in range(NE, 16):
                turn(MK0 + MK1 * (j - NE))
                match(j, PF)
        if c == 5:
            turn(6)
            lists(2, PF)
        if c == 12:
            turn(c)
            lists(3, PF)
            for j in range(4, 16):
                turn(c + (j - 4) / 3)
                flag("pm", "mt", 0, 512, 512 * j, j == 4)
            flag("pn", "inv", 0, 512)
        if n == mine[-1] and t:
            turn(c - 4)
            look(t)
            if t == 2:
                after_two(c)
            if t == 3:
                for s in range(3):
                    seps(s)
                turn(c + 2.3)
                after_three()
        consume(n, c, n == mine[-1])
        seen.append(n)
        if n == mine[-1]:
            turn(c - 1)
            decide(t)
    turn(len(UNITS) + 1)
    seps(3)
    ts(R("sepo"), R("psW", 0, 32), 4096.0, OP.add)
    turn(len(UNITS) + 2)
    HW = R("hw")
    gather("a", R("ru"), HW, R("xl", 0, 24))
    gather_op(R("mg", 1536, 1920), HW, R("xl", 24, 48), R("mt", 1536, 1920), OP.is_lt)
    for c, (base, step) in enumerate(places):
        mm(R("psF", 384, 512), blk("gq", c, 128), R("hw", base, base + 128 * step, step), False, False)
    flag("pn", "eqs", 384, 512)
    flag("pn3", "ru", 0, 384)
    flag("pm", "mg", 0, 384, 1536, False, True)
    ts(R("fl"), PF, 512.0, OP.is_gt)
    k = len(links) // 4
    tr = [RemoteDMATransfer(dst_ids=[dst(q)], dma_engine_mask=some(links[n * k:n * k + k]), remote_sem=T.sem.far,
                            srcs=[ap(blk("fl", q, 128))], dsts=[ap(blk("flin", r, 128))]) for n, q in enumerate(others)]
    remote("far", tr, 3 * k, 3 * k, [R("fl")], [blk("flin", q, 128) for q in others], 3.5)
    for n, q in enumerate([r] + others):
        src = blk("fl" if q == r else "flin", q, 128)
        dma("a" if n % 2 else "s", "oflag", T.yflag[32 * q:32 * q + 32, :], ap(src), [src], [])
    tr = [RemoteDMATransfer(dst_ids=[dst(q) for q in others], dma_engine_mask=wide, remote_sem=T.sem.sar,
                            srcs=[ap(R("sepo"))], dsts=[ap(blk("sepin", r, 32)) for _ in others])]
    remote("sar", tr, len(links), 3 * len(links), [R("sepo")], [blk("sepin", q, 32) for q in others], 3.5)
    for q in range(NR):
        src = R("sepo") if q == r else blk("sepin", q, 32)
        dma("s", "osep", T.ysep[2 * q:2 * q + 2, :], ap(src), [src], [])

    cnt, snap, recs = {}, {}, {}
    clock = {e: {} for e in eng}

    def wait(e, sem, val, isdma):
        if isdma:
            val = cnt[sem]
        if clock[e].get(sem, 0) >= val:
            return
        eng[e].wait_ge(T.sem[sem], val)
        for k, v in snap.get(sem if isdma else (sem, val), {}).items():
            if clock[e].get(k, 0) < v:
                clock[e][k] = v
        clock[e][sem] = max(clock[e].get(sem, 0), val)

    for x in schedule(tasks, bonus):
        e, kind, fn, sem, inc, reads, writes, _, _ = tasks[x]
        isdma = kind != "op"
        if kind != "land":
            best = {}
            for isw, rgs in ((False, reads), (True, writes)):
                for buf, a, b, pm in rgs:
                    for c0, c1, p2, w, e2, s2, v2, d2 in recs.get(buf, []):
                        if c0 >= b or a >= c1 or not pm & p2:
                            continue
                        if not isw and not w and not (buf.startswith("ps") and e2 != e):
                            continue
                        if isw and e2 == e == "p":
                            continue
                        if s2 not in best or best[s2][0] < v2:
                            best[s2] = (v2, d2)
            if e == "g" and kind == "op" and cnt.get("cg"):
                best["cg"] = (cnt["cg"], False)
            for s2 in sorted(best, key=lambda z: (best[z][1], z)):
                wait(e, s2, best[s2][0], best[s2][1])
        cnt[sem] = cnt.get(sem, 0) + inc
        if kind == "send":
            fn(eng[e])
            continue
        if kind != "land":
            fn(eng[e]).then_inc(T.sem[sem], inc)
            if kind == "op":
                sn = dict(clock[e])
                sn[sem] = cnt[sem]
                snap[(sem, cnt[sem])] = sn
            else:
                sn = snap.setdefault(sem, {})
                for k, v in clock[e].items():
                    sn[k] = max(sn.get(k, 0), v)
        for buf, a, b, pm in writes:
            if buf.startswith("token"):
                continue
            lst = recs.setdefault(buf, [])
            lst[:] = [q for q in lst if not (a <= q[0] and q[1] <= b and not q[2] & ~pm)]
            lst.append((a, b, pm, True, e, sem, cnt[sem], isdma))
        for buf, a, b, pm in reads:
            if buf.startswith("token"):
                continue
            lst = recs.setdefault(buf, [])
            lst[:] = [q for q in lst if not (not q[3] and q[5] == sem and a <= q[0] and q[1] <= b and not q[2] & ~pm)]
            lst.append((a, b, pm, False, e, sem, cnt[sem], isdma))

    for sem, val in cnt.items():
        if clock["g"].get(sem, 0) < val:
            g.wait_ge(T.sem[sem], val)
            clock["g"][sem] = val


def schedule(tasks, bonus):
    n = len(tasks)
    deps = [set() for _ in range(n)]
    recs, group = {}, {}
    for x in range(n):
        e, kind, _, sem, _, reads, writes, _, _ = tasks[x]
        for isw, rgs in ((False, reads), (True, writes)):
            for buf, a, b, pm in rgs:
                for c0, c1, p2, w, e2, y in recs.get(buf, []):
                    if c0 < b and a < c1 and pm & p2 and (isw or w or (buf.startswith("ps") and e2 != e)):
                        deps[x].add(y)
        for y in list(deps[x]):
            if tasks[y][1] == "dma":
                deps[x].update(z for z in group[tasks[y][3]] if z < x)
        if kind == "dma":
            group.setdefault(sem, []).append(x)
        for buf, a, b, pm in writes:
            lst = recs.setdefault(buf, [])
            lst[:] = [q for q in lst if not (a <= q[0] and q[1] <= b and not q[2] & ~pm)]
            lst.append((a, b, pm, True, e, x))
        for buf, a, b, pm in reads:
            recs.setdefault(buf, []).append((a, b, pm, False, e, x))
        deps[x].discard(x)
    succ = [[] for _ in range(n)]
    for x in range(n):
        for y in deps[x]:
            succ[y].append(x)
    prio = [0.0] * n
    for x in range(n - 1, -1, -1):
        prio[x] = tasks[x][8] + WAKE + max([prio[y] for y in succ[x]], default=0.0)
    prio = [prio[x] + bonus[x] if bonus[x] >= 0 else bonus[x] for x in range(n)]
    left = [len(deps[x]) for x in range(n)]
    at = [0.0] * n
    free = {}
    ready = {}
    for x in range(n):
        if not left[x]:
            ready.setdefault(tasks[x][0], []).append(x)
    order = []
    while len(order) < n:
        pick = None
        for e in sorted(ready, key=str):
            lst = ready[e]
            if not lst:
                continue
            f = free.get(e, 0.0)
            s0 = min(max(f, at[x]) for x in lst)
            if pick is None or s0 < pick[0]:
                pick = (s0, e)
        s0, e = pick
        x = max((y for y in ready[e] if max(free.get(e, 0.0), at[y]) <= s0 + 0.05), key=lambda y: (prio[y], -y))
        ready[e].remove(x)
        st = max(free.get(e, 0.0), at[x])
        if e is not None:
            free[e] = st + tasks[x][7]
        end = st + tasks[x][8] + WAKE
        order.append(x)
        for y in succ[x]:
            at[y] = max(at[y], end - WAKE if e == tasks[y][0] == "p" else end)
            left[y] -= 1
            if not left[y]:
                ready.setdefault(tasks[y][0], []).append(y)
    return order
